import numpy as np
import ml_dtypes


def mxq(x, axis, fmt="e4m3"):
    dtype, down = {"e4m3": (ml_dtypes.float8_e4m3fn, 7), "e5m2": (ml_dtypes.float8_e5m2, 14)}[fmt]
    v = np.moveaxis(np.asarray(x, np.float32).astype(ml_dtypes.bfloat16).astype(np.float64), axis, -1)
    blocks = v.reshape(v.shape[:-1] + (-1, 32))
    amax = np.abs(blocks).max(-1, keepdims=True)
    byte = np.maximum(np.where(amax > 0, np.frexp(amax)[1] - 1 + 127, 0) - down, 1)
    scale = np.exp2(byte - 127.0)
    codes = (blocks / scale).astype(np.float32).astype(dtype).astype(np.float64)
    return np.moveaxis((codes * scale).reshape(v.shape), -1, axis)


WIDE = False


def mx_kscale(k):
    if not WIDE:
        return np.ones(k)
    levels = np.array([10, -10, 5, -5, 0])
    if k % 512:
        return np.exp2(np.random.permutation(np.resize(levels, k // 32))).repeat(32)
    a = np.empty((k // 512, 16))
    for p in range(k // 512):
        a[p, :8] = np.random.permutation(np.resize(levels, 8))
        for g in range(8):
            far = levels[np.abs(levels - a[p, g]) >= 10]
            a[p, g + 8] = far[np.random.randint(len(far))]
    return np.exp2(a.ravel()).repeat(32)


BF16 = ml_dtypes.bfloat16


def bf(x):
    return np.asarray(x, np.float32).astype(BF16)


def f64(x):
    return np.asarray(x).astype(np.float64)


E2M1 = np.array([0.0, 0.5, 1.0, 1.5, 2.0, 3.0, 4.0, 6.0, -0.0, -0.5, -1.0, -1.5, -2.0, -3.0, -4.0, -6.0])


def pack_weight(w, fmt):
    k, n = w.shape
    w = f64(bf(w)).reshape(k // 32, 32, n)
    amax = np.abs(w).max(1)
    if fmt == "e4m3":
        byte = np.frexp(amax)[1] - 1 + 127 - 7
    else:
        mant, ex = np.frexp(amax / 6.0)
        byte = np.where(mant > 0.5, ex, ex - 1) + 127
    byte = np.clip(np.where(amax > 0, byte, 1), 1, 254)
    scaled = (w * np.exp2(127.0 - byte)[:, None, :]).reshape(k, n).astype(np.float32)
    by_word = np.ascontiguousarray(scaled.reshape(k // 512, 128, 4, n).transpose(0, 1, 3, 2))
    if fmt == "e4m3":
        words = by_word.astype(ml_dtypes.float8_e4m3fn).view(np.uint8)
    else:
        c = by_word.astype(ml_dtypes.float4_e2m1fn).view(np.uint8) & 0xF
        words = c[..., 0::2] | (c[..., 1::2] << 4)
    return np.ascontiguousarray(words), np.ascontiguousarray(byte.astype(np.uint8).reshape(k // 512, 16, n))


def unpack_weight(words, scales, fmt):
    g, p, n, _ = words.shape
    if fmt == "e4m3":
        vals = np.ascontiguousarray(words).view(ml_dtypes.float8_e4m3fn).astype(np.float64)
    else:
        nib = np.empty((g, p, n, 4), np.uint8)
        nib[..., 0::2] = words & 0xF
        nib[..., 1::2] = words >> 4
        vals = E2M1[nib]
    vals = vals * np.repeat(np.exp2(scales.astype(np.float64) - 127.0), 8, axis=1)[..., None]
    return vals.transpose(0, 1, 3, 2).reshape(g * 512, n)
def pack4(w):
    words, scales = pack_weight(w, "e2m1")
    return words.reshape(words.shape[0], 128, -1), scales


def unpack4(words, scales):
    return unpack_weight(words.reshape(words.shape[0], 128, -1, 2), scales, "e2m1")


def planes(Y):
    n, m = Y.shape
    b = f64(bf(Y)).reshape(n // 32, 32, m)
    amax = np.abs(b).max(1)
    byte = np.clip(np.where(amax > 0, np.frexp(amax)[1] - 1 + 127 - 7, 1), 1, 254)
    codes = (b * np.exp2(127.0 - byte)[:, None, :]).reshape(n, m).astype(np.float32).astype(ml_dtypes.float8_e4m3fn).view(np.uint8)
    words = codes.reshape(n // 512, 128, 4, m).transpose(0, 1, 3, 2)
    return np.ascontiguousarray(words), np.ascontiguousarray(byte.astype(np.uint8).reshape(n // 512, 16, m))


P, Q, T = 2048, 1024, 512

SPREAD = 0.8
NORM = 0.95


def setup_inputs():
    s = mx_kscale(Q)
    t = mx_kscale(P)
    a = NORM * np.random.randn(P, Q) / np.sqrt(P)
    v = bf(np.exp(SPREAD * np.random.randn(Q, 1)) * np.random.randn(Q, T))
    x_words, x_scales = pack_weight(f64(v) * s[:, None], "e4m3")
    a4_words, a4_scales = pack4(a.T / s[:, None] * t[None, :])
    return {"x_words": x_words, "x_scales": x_scales,
            "a4_words": a4_words, "a4_scales": a4_scales,
            "a": bf(a / t[:, None]), "v": v}


def reference(x_words, x_scales, a4_words, a4_scales, a, v):
    x = unpack_weight(x_words, x_scales, "e4m3")
    w = unpack4(a4_words, a4_scales)
    h = 0.5 * (w.T @ x)
    hq = mxq(h, 0, "e4m3")
    aq = mxq(f64(a), 0, "e4m3")
    y = 1.5 * f64(v) - (aq.T @ hq)
    Y = y
    words, scales = planes(Y)
    return y, words, scales

@@ -1,0 +1,450 @@
+from contextlib import ExitStack
+
+import concourse.mybir as mybir
+
+F32 = mybir.dt.float32
+BF16 = mybir.dt.bfloat16
+I32 = mybir.dt.int32
+U32 = mybir.dt.uint32
+U8 = mybir.dt.uint8
+FP8X4 = mybir.dt.float8_e4m3fn_x4
+FP4X4 = mybir.dt.float4_e2m1fn_x4
+ALU = mybir.AluOpType
+ACT = mybir.ActivationFunctionType
+
+FLOPS = 2 * 2 * 2048 * 1024 * 512
+
+PROGRAM = [
+    ('ms', 'G', 'msx', 256),
+    ('ldxs', 'G', 0),
+    ('ms', 'V', 'msw', 1024),
+    ('lda', 'SP', 0, 0, (0,)),
+    ('act0',),
+    ('lda', 'SP', 0, 1, (0,)),
+    ('lda', 'SP', 0, 2, (0,)),
+    ('lda', 'SP', 0, 3, (0,)),
+    ('ldx', 'SP'),
+    ('ldw', 'SP', (0,)),
+    ('ldxs', 'G', 1),
+    ('wuq', 512),
+    ('ldws', 'SP', 0, (0, 1)),
+    ('ldws', 'SP', 1, (0, 1)),
+    ('ldxs', 'G', 2),
+    ('wu', 512, 8, 7),
+    ('ldxs', 'G', 3),
+    ('ldws', 'SP', 2, (0, 1)),
+    ('ldws', 'SP', 3, (0, 1)),
+    ('ldw', 'SP', (1,)),
+    ('lda', 'SP', 0, 0, (1,)),
+    ('il', 'S', 0, 0, 2, 4),
+    ('il', 'S', 0, 0, 4, 6),
+    ('lda', 'SP', 0, 1, (1,)),
+    ('il', 'S', 0, 0, 6, 8),
+    ('lda', 'SP', 0, 2, (1,)),
+    ('pw', 0),
+    ('lda', 'SP', 0, 3, (1,)),
+    ('il', 'S', 0, 0, 0, 2),
+    ('ldws', 'SP', 0, (2, 3)),
+    ('ldws', 'SP', 1, (2, 3)),
+    ('ldws', 'SP', 2, (2, 3)),
+    ('ps', (0, 1)),
+    ('qa', 0, 0),
+    ('s1', 0, 0, 0),
+    ('ldws', 'SP', 3, (2, 3)),
+    ('lda', 'SP', 1, 0, (0, 1)),
+    ('pw', 1),
+    ('lda', 'SP', 1, 1, (0, 1)),
+    ('s1', 0, 1, 1),
+    ('lda', 'SP', 1, 2, (0, 1)),
+    ('ev', 'S', 0, 0, 0),
+    ('lda', 'SP', 1, 3, (0, 1)),
+    ('il', 'V', 0, 1, 0, 2),
+    ('ldw', 'SP', (2,)),
+    ('s1', 0, 2, 2),
+    ('ldw', 'SP', (3,)),
+    ('il', 'V', 0, 1, 2, 4),
+    ('ev', 'S', 0, 1, 1),
+    ('lda', 'SP', 2, 0, (0, 1)),
+    ('il', 'V', 0, 1, 4, 6),
+    ('s1', 0, 3, 3),
+    ('lda', 'SP', 2, 1, (0, 1)),
+    ('ps', (2, 3)),
+    ('ev', 'S', 0, 2, 2),
+    ('qh', 0, [0, 1]),
+    ('s1', 1, 0, 4),
+    ('lda', 'SP', 2, 2, (0, 1)),
+    ('il', 'V', 0, 1, 6, 8),
+    ('ev', 'S', 0, 3, 3),
+    ('lda', 'SP', 2, 3, (0, 1)),
+    ('s1', 1, 1, 5),
+    ('qa', 0, 1),
+    ('ev', 'S', 1, 0, 4),
+    ('lda', 'SP', 3, 0, (0, 1)),
+    ('s1', 1, 2, 6),
+    ('qh', 0, [2, 3]),
+    ('ev', 'S', 1, 1, 5),
+    ('lda', 'SP', 3, 1, (0, 1)),
+    ('il', 'V', 1, 0, 0, 2),
+    ('s1', 1, 3, 7),
+    ('il', 'V', 1, 1, 4, 6),
+    ('ev', 'S', 1, 2, 6),
+    ('lda', 'SP', 3, 2, (0, 1)),
+    ('pw', 2),
+    ('il', 'V', 1, 0, 2, 4),
+    ('lda', 'SP', 3, 3, (0, 1)),
+    ('ev', 'S', 1, 3, 7),
+    ('s1', 2, 0, 0),
+    ('qh', 1, [0, 1]),
+    ('ldv', 'SP', (0,)),
+    ('pw', 3),
+    ('il', 'S', 1, 1, 0, 2),
+    ('s1', 2, 1, 1),
+    ('il', 'V', 1, 0, 6, 8),
+    ('ldv', 'SP', (1,)),
+    ('qh', 1, [2, 3]),
+    ('ev', 'S', 2, 0, 0),
+    ('s1', 2, 2, 2),
+    ('il', 'V', 1, 1, 6, 8),
+    ('il', 'V', 1, 0, 4, 6),
+    ('ev', 'S', 2, 1, 1),
+    ('s1', 2, 3, 3),
+    ('il', 'V', 2, 0, 4, 6),
+    ('ev', 'S', 2, 2, 2),
+    ('qa', 1, 0),
+    ('s1', 3, 0, 4),
+    ('ev', 'S', 2, 3, 3),
+    ('il', 'V', 2, 1, 0, 2),
+    ('s1', 3, 1, 5),
+    ('il', 'V', 2, 0, 6, 8),
+    ('il', 'S', 2, 0, 2, 4),
+    ('qh', 2, [2, 3]),
+    ('s1', 3, 2, 6),
+    ('qh', 2, [0, 1]),
+    ('ev', 'S', 3, 1, 5),
+    ('il', 'V', 3, 0, 0, 2),
+    ('s1', 3, 3, 7),
+    ('il', 'V', 3, 0, 4, 6),
+    ('ev', 'S', 3, 0, 4),
+    ('il', 'V', 2, 0, 0, 2),
+    ('s2', 0, 0, 0, [0, 1], 0, 0),
+    ('il', 'S', 3, 0, 2, 4),
+    ('il', 'V', 3, 0, 6, 8),
+    ('s2', 0, 0, 1, [0, 1], 1, 0),
+    ('s2', 0, 0, 2, [0, 1], 2, 0),
+    ('s2', 0, 0, 3, [0, 1], 3, 0),
+    ('qh', 3, [0, 1]),
+    ('s2', 0, 1, 0, [0, 1], 0, 0),
+    ('s2', 0, 1, 1, [0, 1], 1, 0),
+    ('ev', 'S', 3, 3, 7),
+    ('qa', 2, 0),
+    ('s2', 0, 1, 2, [0, 1], 2, 0),
+    ('s2', 0, 1, 3, [0, 1], 3, 0),
+    ('ev', 'S', 3, 2, 6),
+    ('qa', 3, 0),
+    ('s2', 0, 2, 0, [0, 1], 0, 0),
+    ('s2', 0, 2, 1, [0, 1], 1, 0),
+    ('s2', 0, 2, 2, [0, 1], 2, 0),
+    ('il', 'S', 2, 1, 4, 6),
+    ('il', 'V', 1, 1, 2, 4),
+    ('s2', 0, 2, 3, [0, 1], 3, 0),
+    ('s2', 0, 3, 0, [0, 1], 0, 0),
+    ('qh', 3, [2, 3]),
+    ('s2', 0, 3, 1, [0, 1], 1, 0),
+    ('s2', 0, 3, 2, [0, 1], 2, 0),
+    ('il', 'S', 3, 1, 4, 6),
+    ('s2', 0, 3, 3, [0, 1], 3, 0),
+    ('qa', 1, 1),
+    ('s2', 0, 0, 0, [2, 3], 4, 0),
+    ('s2', 0, 1, 0, [2, 3], 4, 0),
+    ('s2', 0, 2, 0, [2, 3], 4, 0),
+    ('s2', 0, 3, 0, [2, 3], 4, 0),
+    ('stt', 0, [3], [0, 1], 3, 0),
+    ('il', 'S', 3, 1, 2, 4),
+    ('s2', 0, 0, 1, [2, 3], 5, 0),
+    ('s2', 0, 1, 1, [2, 3], 5, 0),
+    ('stt', 0, [1], [0, 1], 1, 0),
+    ('s2', 0, 2, 1, [2, 3], 5, 0),
+    ('s2', 0, 3, 1, [2, 3], 5, 0),
+    ('stt', 0, [0], [0, 1], 0, 0),
+    ('s2', 0, 0, 2, [2, 3], 6, 0),
+    ('il', 'S', 2, 1, 2, 4),
+    ('s2', 0, 1, 2, [2, 3], 6, 0),
+    ('stt', 0, [1], [2, 3], 5, 0),
+    ('s2', 0, 2, 2, [2, 3], 6, 0),
+    ('s2', 0, 3, 2, [2, 3], 6, 0),
+    ('s2', 0, 0, 3, [2, 3], 7, 0),
+    ('stt', 0, [2], [0, 1], 2, 0),
+    ('il', 'S', 2, 1, 6, 8),
+    ('s2', 0, 1, 3, [2, 3], 7, 0),
+    ('s2', 0, 2, 3, [2, 3], 7, 0),
+    ('stt', 0, [2], [2, 3], 6, 0),
+    ('s2', 0, 3, 3, [2, 3], 7, 0),
+    ('s2', 1, 0, 0, [0, 1], 0, 0),
+    ('sty', 'SP', 0, [0, 1, 2, 3], [0, 1]),
+    ('cast', 'V', 0, 2, 4),
+    ('s2', 1, 0, 1, [0, 1], 1, 0),
+    ('cast', 'S', 0, 6, 8),
+    ('il', 'V', 3, 1, 0, 2),
+    ('s2', 1, 0, 2, [0, 1], 2, 0),
+    ('s2', 1, 0, 3, [0, 1], 3, 0),
+    ('s2', 1, 1, 0, [0, 1], 0, 0),
+    ('il', 'S', 3, 1, 6, 8),
+    ('qa', 2, 1),
+    ('s2', 1, 1, 1, [0, 1], 1, 0),
+    ('s2', 1, 1, 2, [0, 1], 2, 0),
+    ('s2', 1, 1, 3, [0, 1], 3, 0),
+    ('stt', 0, [0], [2, 3], 4, 0),
+    ('cast', 'S', 0, 0, 2),
+    ('s2', 1, 2, 0, [0, 1], 0, 0),
+    ('qa', 3, 1),
+    ('cast', 'S', 0, 4, 6),
+    ('s2', 1, 2, 1, [0, 1], 1, 0),
+    ('s2', 1, 2, 2, [0, 1], 2, 0),
+    ('s2', 1, 2, 3, [0, 1], 3, 0),
+    ('stt', 0, [3], [2, 3], 7, 0),
+    ('s2', 1, 3, 0, [0, 1], 0, 0),
+    ('qy', 0, [0, 1]),
+    ('s2', 1, 3, 1, [0, 1], 1, 0),
+    ('s2', 1, 3, 2, [0, 1], 2, 0),
+    ('sty', 'SP', 0, [0, 1, 2, 3], [2, 3]),
+    ('cast', 'S', 0, 8, 10),
+    ('cast', 'V', 0, 10, 12),
+    ('s2', 1, 3, 3, [0, 1], 3, 0),
+    ('s2', 1, 0, 0, [2], 4, 0),
+    ('stt', 1, [1], [0, 1], 1, 0),
+    ('cast', 'S', 0, 14, 16),
+    ('s2', 1, 1, 0, [2], 4, 0),
+    ('s2', 1, 2, 0, [2], 4, 0),
+    ('s2', 1, 3, 0, [2], 4, 0),
+    ('stt', 1, [2], [0, 1], 2, 0),
+    ('s2', 1, 0, 1, [2], 5, 0),
+    ('s2', 1, 1, 1, [2], 5, 0),
+    ('cast', 'S', 0, 12, 14),
+    ('s2', 1, 2, 1, [2], 5, 0),
+    ('s2', 1, 3, 1, [2], 5, 0),
+    ('stt', 1, [0], [0, 1], 0, 0),
+    ('s2', 1, 0, 2, [2], 6, 0),
+    ('s2', 1, 1, 2, [2], 6, 0),
+    ('s2', 1, 2, 2, [2], 6, 0),
+    ('s2', 1, 3, 2, [2], 6, 0),
+    ('s2', 1, 0, 3, [2], 7, 0),
+    ('qy', 0, [2, 3]),
+    ('s2', 1, 1, 3, [2], 7, 0),
+    ('s2', 1, 2, 3, [2], 7, 0),
+    ('s2', 1, 3, 3, [2], 7, 0),
+    ('s2', 1, 0, 0, [3], 0, 0),
+    ('stt', 1, [1], [2], 5, 0),
+    ('s2', 1, 1, 0, [3], 0, 0),
+    ('s2', 1, 2, 0, [3], 0, 0),
+    ('s2', 1, 3, 0, [3], 0, 0),
+    ('stq', 'SP', 0, [0, 1, 2, 3]),
+    ('stt', 1, [3], [2], 7, 0),
+    ('s2', 1, 0, 1, [3], 1, 0),
+    ('s2', 1, 1, 1, [3], 1, 0),
+    ('stt', 1, [3], [0, 1], 3, 0),
+    ('s2', 1, 2, 1, [3], 1, 0),
+    ('s2', 1, 3, 1, [3], 1, 0),
+    ('s2', 1, 0, 2, [3], 2, 0),
+    ('s2', 1, 1, 2, [3], 2, 0),
+    ('stt', 1, [0], [2], 4, 0),
+    ('s2', 1, 2, 2, [3], 2, 0),
+    ('s2', 1, 3, 2, [3], 2, 0),
+    ('sty', 'SP', 1, [0, 1, 2, 3], [0, 1]),
+    ('cast', 'S', 1, 4, 6),
+    ('s2', 1, 0, 3, [3], 3, 0),
+    ('cast', 'V', 1, 0, 2),
+    ('s2', 1, 1, 3, [3], 3, 0),
+    ('s2', 1, 2, 3, [3], 3, 0),
+    ('stt', 1, [2], [3], 2, 0),
+    ('s2', 1, 3, 3, [3], 3, 0),
+    ('cast', 'S', 1, 2, 4),
+    ('stt', 1, [2], [2], 6, 0),
+    ('stt', 1, [1], [3], 1, 0),
+    ('cast', 'S', 1, 6, 8),
+    ('stt', 1, [0], [3], 0, 0),
+    ('sty', 'SP', 1, [0, 1, 2, 3], [2]),
+    ('stt', 1, [3], [3], 3, 0),
+    ('cast', 'S', 1, 8, 10),
+    ('qy', 1, [0, 1]),
+    ('cast', 'S', 1, 10, 12),
+    ('cast', 'V', 1, 12, 14),
+    ('cast', 'V', 1, 14, 16),
+    ('stq', 'SP', 1, [0, 1]),
+    ('sty', 'SP', 1, [0, 1, 2, 3], [3]),
+    ('qy', 1, [2]),
+    ('qy', 1, [3]),
+    ('stq', 'SP', 1, [2, 3]),
+    ('sts', 'S', (0, 1), 2),
+    ('sts', 'S', (0, 1), 0),
+    ('sts', 'SP', (0, 1), 1),
+    ('sts', 'SP', (0, 1), 3),
+
+]
+
+
+def tile_newton_schulz_factor_block_h2_kernel(tc, x_words, x_scales, a4_words, a4_scales, a, v, out_0, out_1, out_2):
+    nc = tc.nc
+    eng = {"V": nc.vector, "S": nc.scalar, "SP": nc.sync, "G": nc.gpsimd}
+    with ExitStack() as ctx:
+        sb = ctx.enter_context(tc.tile_pool(name="sb", bufs=1))
+        ps = ctx.enter_context(tc.psum_pool(name="ps", bufs=1))
+        x_codes = sb.tile([128, 2, 512], U32, align_bytes=256)
+        x_sc = sb.tile([128, 2, 512], U8, align_bytes=256)
+        w_raw = sb.tile([128, 4, 2, 1024], U8, align_bytes=256)
+        w_perm = sb.tile([128, 4, 4, 2, 256], U8, align_bytes=256)
+        ws_raw = sb.tile([128, 2, 2048], U8, align_bytes=256)
+        ws_perm = sb.tile([128, 2, 4, 4, 128], U8, align_bytes=256)
+        a_raw = sb.tile([128, 4, 4, 1024], BF16, align_bytes=256)
+        a_il = sb.tile([128, 4, 2, 2048], BF16, align_bytes=256)
+        a_codes = sb.tile([128, 4, 2, 512], U32, align_bytes=256)
+        a_sc = sb.tile([128, 4, 2, 512], U8, align_bytes=256)
+        h_il = sb.tile([128, 4, 2048], BF16, align_bytes=256)
+        h_codes = sb.tile([128, 4, 512], U32, align_bytes=256)
+        h_sc = sb.tile([128, 4, 512], U8, align_bytes=256)
+        v_sb = sb.tile([128, 2, 4, 512], BF16, align_bytes=256)
+        y32 = sb.tile([128, 2, 4, 512], F32, align_bytes=256)
+        y_il = sb.tile([128, 2, 2048], BF16, align_bytes=256)
+        y_codes = sb.tile([128, 2, 512], U32, align_bytes=256)
+        y_sc = sb.tile([128, 2, 512], U8, align_bytes=256)
+        prime = sb.tile([128, 8], F32, align_bytes=256)
+        prime2 = sb.tile([128, 8], F32, align_bytes=256)
+        wu_in = sb.tile([128, 2048], BF16, align_bytes=256)
+        wu_codes = sb.tile([128, 512], U32, align_bytes=256)
+        wu_sc = sb.tile([128, 512], U8, align_bytes=256)
+        banks = {}
+
+        def new_bank(b):
+            banks[b] = ps.tile([128, 512], F32, name="bank%d" % b, tag="bank%d" % b)
+            return banks[b]
+
+        def copy(e, out, in_):
+            if e == "V":
+                nc.vector.tensor_copy(out=out, in_=in_)
+            else:
+                nc.scalar.copy(out=out, in_=in_)
+
+        ctx.enter_context(tc.manual_schedule())
+        for st in PROGRAM:
+            k = st[0]
+            if k == "ms":
+                t = x_sc if st[2] == "msx" else ws_raw
+                eng[st[1]].memset(t[:].rearrange("p g n -> p (g n)").bitcast(I32), 0)
+            elif k == "act0":
+                nc.gpsimd.memset(prime[:], 0.0)
+                nc.scalar.activation(out=prime2[:], in_=prime[:], func=ACT.Copy, scale=0.5)
+            elif k == "wuq":
+                n = st[1]
+                nc.vector.memset(wu_in[:, : 4 * n], 0.0)
+                nc.vector.quantize_mx(out=wu_codes[:, :n].bitcast(FP8X4), scales=wu_sc[:, :n], in_=wu_in[:, : 4 * n])
+            elif k == "wu":
+                n = st[1]
+                bank = new_bank(st[3])
+                for i in range(st[2]):
+                    nc.tensor.matmul_mx(out=bank[:, :n], lhsT=wu_codes[:, :128].bitcast(FP8X4), lhsT_scale=wu_sc[:, :128],
+                                        rhs=wu_codes[:, :n].bitcast(FP8X4), rhs_scale=wu_sc[:, :n], start=True, stop=True)
+            elif k == "ldx":
+                eng[st[1]].dma_start(out=x_codes[:].bitcast(I32), in_=x_words.rearrange("g p n t -> p g (n t)").bitcast(I32))
+            elif k == "ldxs":
+                r = st[2]
+                eng[st[1]].dma_start(out=x_sc[r:128:32, :, :].bitcast(I32),
+                                     in_=x_scales.rearrange("g (q r) n -> r q g n", r=4)[r].bitcast(I32))
+            elif k == "ldws":
+                r = st[2]
+                cols = slice(512 * st[3][0], 512 * (st[3][-1] + 1))
+                eng[st[1]].dma_start(out=ws_raw[r:128:32, :, cols].bitcast(I32),
+                                     in_=a4_scales.rearrange("g (q r) n -> r q g n", r=4)[r][:, :, cols].bitcast(I32))
+            elif k == "ldw":
+                for G in st[2]:
+                    eng[st[1]].dma_start(out=w_raw[:, G, :, :].bitcast(I32),
+                                         in_=a4_words[:, :, 1024 * G : 1024 * (G + 1)].rearrange("g p n -> p g n").bitcast(I32))
+            elif k == "lda":
+                G, t, gs = st[2], st[3], st[4]
+                cols = slice(512 * gs[0], 512 * (gs[-1] + 1))
+                rows = a[512 * G : 512 * (G + 1), :].rearrange("(j t i) q -> t j i q", t=4, i=8)
+                eng[st[1]].dma_start(out=a_raw[:, G, t, cols], in_=rows[t][:, :, cols])
+            elif k == "ldv":
+                for g in st[2]:
+                    eng[st[1]].dma_start(out=v_sb[:, g, :, :], in_=v[512 * g : 512 * (g + 1), :].rearrange("(p t) m -> p t m", t=4))
+            elif k == "pw":
+                G = st[1]
+                src = w_raw[:, G, :, :].rearrange("p g n -> p (g n)").bitcast(I32).rearrange("p (j t i) -> p t j i", t=4, i=4)
+                dst = w_perm[:, G, :, :, :].rearrange("p t g n -> p (t g n)").bitcast(I32).rearrange("p (t j i) -> p t j i", t=4, i=4)
+                nc.vector.tensor_copy(out=dst, in_=src)
+            elif k == "ps":
+                G0, G1 = st[1][0], st[1][-1] + 1
+                for gk in range(2):
+                    src = ws_raw[:, gk, 512 * G0 : 512 * G1].bitcast(I32).rearrange("p (j t i) -> p t j i", t=4, i=2)
+                    dst = ws_perm[:, gk, :, G0:G1, :].rearrange("p t G n -> p t (G n)").bitcast(I32).rearrange("p t (j i) -> p t j i", i=2)
+                    nc.vector.tensor_copy(out=dst, in_=src)
+            elif k == "s1":
+                G, c = st[1], st[2]
+                bank = new_bank(st[3])
+                for t in range(4):
+                    for gk in range(2):
+                        nc.tensor.matmul_mx(out=bank[:, 128 * t : 128 * (t + 1)],
+                                            lhsT=w_perm[:, G, t, gk, :].bitcast(FP4X4), lhsT_scale=ws_perm[:, gk, t, G, :],
+                                            rhs=x_codes[:, gk, 128 * c : 128 * (c + 1)].bitcast(FP8X4),
+                                            rhs_scale=x_sc[:, gk, 128 * c : 128 * (c + 1)], start=(gk == 0), stop=(gk == 1))
+            elif k == "ev":
+                e, G, c = st[1], st[2], st[3]
+                src = banks[st[4]][:].rearrange("p (t m) -> p m t", t=4)
+                dst = h_il[:, G, 512 * c : 512 * (c + 1)].rearrange("p (m t) -> p m t", t=4)
+                if e == "S":
+                    nc.scalar.activation(out=dst, in_=src, func=ACT.Copy, scale=0.5)
+                else:
+                    nc.vector.tensor_scalar_mul(out=dst, in0=src, scalar1=0.5)
+            elif k == "il":
+                e, G, g, m0, m1 = st[1], st[2], st[3], 16 * st[4], 16 * st[5]
+                src = a_raw[:, G, :, 512 * g + 4 * m0 : 512 * g + 4 * m1].rearrange("p j (m t) -> p m j t", t=4)
+                dst = a_il[:, G, g, :].rearrange("p (t m j) -> p m j t", t=4, j=4)[:, m0:m1, :, :]
+                copy(e, dst, src)
+            elif k == "qa":
+                G, g = st[1], st[2]
+                nc.vector.quantize_mx(out=a_codes[:, G, g, :].bitcast(FP8X4), scales=a_sc[:, G, g, :], in_=a_il[:, G, g, :])
+            elif k == "qh":
+                G, c0, c1 = st[1], 128 * st[2][0], 128 * (st[2][-1] + 1)
+                nc.vector.quantize_mx(out=h_codes[:, G, c0:c1].bitcast(FP8X4), scales=h_sc[:, G, c0:c1], in_=h_il[:, G, 4 * c0 : 4 * c1])
+            elif k == "s2":
+                g, G, t, cs, b = st[1:6]
+                c0, c1 = 128 * cs[0], 128 * (cs[-1] + 1)
+                n = c1 - c0
+                slot = st[6]
+                if G == 0 and slot == 0:
+                    new_bank(b)
+                nc.tensor.matmul_mx(out=banks[b][:, n * slot : n * (slot + 1)],
+                                    lhsT=a_codes[:, G, g, 128 * t : 128 * (t + 1)].bitcast(FP8X4),
+                                    lhsT_scale=a_sc[:, G, g, 128 * t : 128 * (t + 1)],
+                                    rhs=h_codes[:, G, c0:c1].bitcast(FP8X4), rhs_scale=h_sc[:, G, c0:c1],
+                                    start=(G == 0), stop=(G == 3))
+            elif k == "stt":
+                g, ts, cs, b, off = st[1:6]
+                c0, c1 = 128 * cs[0], 128 * (cs[-1] + 1)
+                n = c1 - c0
+                t0, t1 = ts[0], ts[-1] + 1
+                src = banks[b][:, off : off + n * len(ts)].rearrange("p (t m) -> p t m", t=len(ts))
+                nc.vector.scalar_tensor_tensor(out=y32[:, g, t0:t1, c0:c1], in0=v_sb[:, g, t0:t1, c0:c1], scalar=1.5, in1=src,
+                                               op0=ALU.mult, op1=ALU.subtract)
+            elif k == "cast":
+                e, g, m0, m1 = st[1], st[2], 32 * st[3], 32 * st[4]
+                src = y32[:, g, :, m0:m1].rearrange("p t (c i) -> p c t i", i=4)
+                dst = y_il[:, g, 4 * m0 : 4 * m1].rearrange("p (c i t) -> p c t i", i=4, t=4)
+                copy(e, dst, src)
+            elif k == "qy":
+                g, c0, c1 = st[1], 128 * st[2][0], 128 * (st[2][-1] + 1)
+                nc.vector.quantize_mx(out=y_codes[:, g, c0:c1].bitcast(FP8X4), scales=y_sc[:, g, c0:c1], in_=y_il[:, g, 4 * c0 : 4 * c1])
+            elif k == "sty":
+                g, ts, cs = st[2], st[3], st[4]
+                c0, c1 = 128 * cs[0], 128 * (cs[-1] + 1)
+                t0, t1 = ts[0], ts[-1] + 1
+                dst = out_0[512 * g : 512 * (g + 1), :].rearrange("(p t) m -> p t m", t=4)
+                eng[st[1]].dma_start(out=dst[:, t0:t1, c0:c1], in_=y32[:, g, t0:t1, c0:c1])
+            elif k == "stq":
+                g, c0, c1 = st[2], 128 * st[3][0], 128 * (st[3][-1] + 1)
+                dst = out_1[g].rearrange("p m t -> p (m t)").bitcast(I32)
+                eng[st[1]].dma_start(out=dst[:, c0:c1], in_=y_codes[:, g, c0:c1].bitcast(I32))
+            elif k == "sts":
+                g0, g1, r = st[2][0], st[2][-1] + 1, st[3]
+                dst = out_2.rearrange("g (q r) n -> r q g n", r=4)[r]
+                eng[st[1]].dma_start(out=dst[:, g0:g1, :].bitcast(I32), in_=y_sc[r:128:32, g0:g1, :].bitcast(I32))
+            else:
+                raise ValueError(k)

@@ -15,268 +15,242 @@ ACT = mybir.ActivationFunctionType
 FLOPS = 2 * 2 * 2048 * 1024 * 512
 
 PROGRAM = [
-    ('ms', 'G', 'msx', 256),
-    ('ldxs', 'G', 0),
     ('ms', 'V', 'msw', 1024),
     ('lda', 'SP', 0, 0, (0,)),
     ('act0',),
     ('lda', 'SP', 0, 1, (0,)),
     ('lda', 'SP', 0, 2, (0,)),
     ('lda', 'SP', 0, 3, (0,)),
+    ('ms', 'V', 'msx', 256),
+    ('wuq', 128),
+    ('ldws', 'SP', 0, (0, 1, 2, 3)),
+    ('ldws', 'SP', 1, (0, 1, 2, 3)),
+    ('ldws', 'SP', 2, (0, 1, 2, 3)),
+    ('ldws', 'SP', 3, (0, 1, 2, 3)),
+    ('wu', 128, 30, 7),
     ('ldx', 'SP'),
     ('ldw', 'SP', (0,)),
-    ('ldxs', 'G', 1),
-    ('wuq', 512),
-    ('ldws', 'SP', 0, (0, 1)),
-    ('ldws', 'SP', 1, (0, 1)),
-    ('ldxs', 'G', 2),
-    ('wu', 512, 8, 7),
-    ('ldxs', 'G', 3),
-    ('ldws', 'SP', 2, (0, 1)),
-    ('ldws', 'SP', 3, (0, 1)),
+    ('ldxs', 'SP', 0),
+    ('ldxs', 'SP', 1),
+    ('il', 'V', 0, 0, 0, 4),
+    ('il', 'S', 0, 0, 4, 8),
+    ('ldxs', 'SP', 2),
+    ('ldxs', 'SP', 3),
     ('ldw', 'SP', (1,)),
     ('lda', 'SP', 0, 0, (1,)),
-    ('il', 'S', 0, 0, 2, 4),
-    ('il', 'S', 0, 0, 4, 6),
+    ('ps', (2, 3)),
+    ('ps', (0, 1)),
+    ('qa', 0, 0),
     ('lda', 'SP', 0, 1, (1,)),
-    ('il', 'S', 0, 0, 6, 8),
     ('lda', 'SP', 0, 2, (1,)),
     ('pw', 0),
     ('lda', 'SP', 0, 3, (1,)),
-    ('il', 'S', 0, 0, 0, 2),
-    ('ldws', 'SP', 0, (2, 3)),
-    ('ldws', 'SP', 1, (2, 3)),
-    ('ldws', 'SP', 2, (2, 3)),
-    ('ps', (0, 1)),
-    ('qa', 0, 0),
-    ('s1', 0, 0, 0),
-    ('ldws', 'SP', 3, (2, 3)),
     ('lda', 'SP', 1, 0, (0, 1)),
-    ('pw', 1),
     ('lda', 'SP', 1, 1, (0, 1)),
-    ('s1', 0, 1, 1),
     ('lda', 'SP', 1, 2, (0, 1)),
-    ('ev', 'S', 0, 0, 0),
+    ('s1', 0, 0, 0),
     ('lda', 'SP', 1, 3, (0, 1)),
-    ('il', 'V', 0, 1, 0, 2),
+    ('pw', 1),
     ('ldw', 'SP', (2,)),
-    ('s1', 0, 2, 2),
+    ('s1', 0, 1, 1),
+    ('ev', 'S', 0, 0, 0),
     ('ldw', 'SP', (3,)),
-    ('il', 'V', 0, 1, 2, 4),
-    ('ev', 'S', 0, 1, 1),
+    ('s1', 0, 2, 2),
     ('lda', 'SP', 2, 0, (0, 1)),
-    ('il', 'V', 0, 1, 4, 6),
-    ('s1', 0, 3, 3),
+    ('ev', 'S', 0, 1, 1),
     ('lda', 'SP', 2, 1, (0, 1)),
-    ('ps', (2, 3)),
+    ('il', 'V', 0, 1, 0, 4),
+    ('s1', 0, 3, 3),
     ('ev', 'S', 0, 2, 2),
+    ('lda', 'SP', 2, 2, (0, 1)),
     ('qh', 0, [0, 1]),
     ('s1', 1, 0, 4),
-    ('lda', 'SP', 2, 2, (0, 1)),
-    ('il', 'V', 0, 1, 6, 8),
+    ('il', 'V', 0, 1, 4, 8),
     ('ev', 'S', 0, 3, 3),
     ('lda', 'SP', 2, 3, (0, 1)),
     ('s1', 1, 1, 5),
-    ('qa', 0, 1),
-    ('ev', 'S', 1, 0, 4),
     ('lda', 'SP', 3, 0, (0, 1)),
-    ('s1', 1, 2, 6),
+    ('ev', 'S', 1, 0, 4),
     ('qh', 0, [2, 3]),
-    ('ev', 'S', 1, 1, 5),
+    ('s1', 1, 2, 6),
     ('lda', 'SP', 3, 1, (0, 1)),
-    ('il', 'V', 1, 0, 0, 2),
+    ('il', 'V', 1, 1, 0, 4),
+    ('il', 'S', 1, 0, 0, 4),
     ('s1', 1, 3, 7),
-    ('il', 'V', 1, 1, 4, 6),
-    ('ev', 'S', 1, 2, 6),
     ('lda', 'SP', 3, 2, (0, 1)),
     ('pw', 2),
-    ('il', 'V', 1, 0, 2, 4),
+    ('il', 'V', 1, 0, 4, 8),
     ('lda', 'SP', 3, 3, (0, 1)),
-    ('ev', 'S', 1, 3, 7),
     ('s1', 2, 0, 0),
-    ('qh', 1, [0, 1]),
+    ('ev', 'S', 1, 3, 7),
     ('ldv', 'SP', (0,)),
     ('pw', 3),
-    ('il', 'S', 1, 1, 0, 2),
     ('s1', 2, 1, 1),
-    ('il', 'V', 1, 0, 6, 8),
+    ('qa', 1, 0),
+    ('ev', 'S', 1, 2, 6),
     ('ldv', 'SP', (1,)),
-    ('qh', 1, [2, 3]),
-    ('ev', 'S', 2, 0, 0),
     ('s1', 2, 2, 2),
-    ('il', 'V', 1, 1, 6, 8),
-    ('il', 'V', 1, 0, 4, 6),
+    ('qa', 0, 1),
+    ('ev', 'S', 1, 1, 5),
+    ('qh', 1, [2, 3]),
     ('ev', 'S', 2, 1, 1),
     ('s1', 2, 3, 3),
-    ('il', 'V', 2, 0, 4, 6),
+    ('il', 'V', 2, 0, 4, 8),
     ('ev', 'S', 2, 2, 2),
-    ('qa', 1, 0),
     ('s1', 3, 0, 4),
+    ('qh', 1, [0, 1]),
     ('ev', 'S', 2, 3, 3),
-    ('il', 'V', 2, 1, 0, 2),
+    ('il', 'V', 2, 0, 0, 4),
     ('s1', 3, 1, 5),
-    ('il', 'V', 2, 0, 6, 8),
-    ('il', 'S', 2, 0, 2, 4),
-    ('qh', 2, [2, 3]),
+    ('ev', 'S', 2, 0, 0),
     ('s1', 3, 2, 6),
-    ('qh', 2, [0, 1]),
+    ('qh', 2, [2, 3]),
     ('ev', 'S', 3, 1, 5),
-    ('il', 'V', 3, 0, 0, 2),
+    ('qa', 2, 0),
     ('s1', 3, 3, 7),
-    ('il', 'V', 3, 0, 4, 6),
-    ('ev', 'S', 3, 0, 4),
-    ('il', 'V', 2, 0, 0, 2),
+    ('il', 'S', 3, 0, 4, 8),
+    ('qh', 2, [0, 1]),
+    ('il', 'V', 3, 0, 0, 4),
     ('s2', 0, 0, 0, [0, 1], 0, 0),
-    ('il', 'S', 3, 0, 2, 4),
-    ('il', 'V', 3, 0, 6, 8),
     ('s2', 0, 0, 1, [0, 1], 1, 0),
     ('s2', 0, 0, 2, [0, 1], 2, 0),
     ('s2', 0, 0, 3, [0, 1], 3, 0),
-    ('qh', 3, [0, 1]),
     ('s2', 0, 1, 0, [0, 1], 0, 0),
+    ('il', 'V', 1, 1, 4, 8),
     ('s2', 0, 1, 1, [0, 1], 1, 0),
     ('ev', 'S', 3, 3, 7),
-    ('qa', 2, 0),
     ('s2', 0, 1, 2, [0, 1], 2, 0),
     ('s2', 0, 1, 3, [0, 1], 3, 0),
-    ('ev', 'S', 3, 2, 6),
-    ('qa', 3, 0),
     ('s2', 0, 2, 0, [0, 1], 0, 0),
     ('s2', 0, 2, 1, [0, 1], 1, 0),
+    ('qa', 3, 0),
+    ('ev', 'S', 3, 0, 4),
     ('s2', 0, 2, 2, [0, 1], 2, 0),
-    ('il', 'S', 2, 1, 4, 6),
-    ('il', 'V', 1, 1, 2, 4),
     ('s2', 0, 2, 3, [0, 1], 3, 0),
-    ('s2', 0, 3, 0, [0, 1], 0, 0),
+    ('qa', 1, 1),
+    ('ev', 'S', 3, 2, 6),
+    ('qh', 3, [0, 1]),
+    ('il', 'S', 2, 1, 4, 8),
     ('qh', 3, [2, 3]),
+    ('s2', 0, 3, 0, [0, 1], 0, 0),
+    ('il', 'V', 2, 1, 0, 4),
     ('s2', 0, 3, 1, [0, 1], 1, 0),
     ('s2', 0, 3, 2, [0, 1], 2, 0),
-    ('il', 'S', 3, 1, 4, 6),
     ('s2', 0, 3, 3, [0, 1], 3, 0),
-    ('qa', 1, 1),
     ('s2', 0, 0, 0, [2, 3], 4, 0),
     ('s2', 0, 1, 0, [2, 3], 4, 0),
+    ('stt', 0, [1], [0, 1], 1, 0),
+    ('il', 'S', 3, 1, 0, 4),
     ('s2', 0, 2, 0, [2, 3], 4, 0),
     ('s2', 0, 3, 0, [2, 3], 4, 0),
-    ('stt', 0, [3], [0, 1], 3, 0),
-    ('il', 'S', 3, 1, 2, 4),
+    ('stt', 0, [2], [0, 1], 2, 0),
     ('s2', 0, 0, 1, [2, 3], 5, 0),
     ('s2', 0, 1, 1, [2, 3], 5, 0),
-    ('stt', 0, [1], [0, 1], 1, 0),
+    ('stt', 0, [0], [0, 1], 0, 0),
     ('s2', 0, 2, 1, [2, 3], 5, 0),
     ('s2', 0, 3, 1, [2, 3], 5, 0),
-    ('stt', 0, [0], [0, 1], 0, 0),
     ('s2', 0, 0, 2, [2, 3], 6, 0),
-    ('il', 'S', 2, 1, 2, 4),
+    ('stt', 0, [0], [2, 3], 4, 0),
     ('s2', 0, 1, 2, [2, 3], 6, 0),
-    ('stt', 0, [1], [2, 3], 5, 0),
     ('s2', 0, 2, 2, [2, 3], 6, 0),
+    ('stt', 0, [1], [2, 3], 5, 0),
+    ('il', 'S', 3, 1, 4, 8),
     ('s2', 0, 3, 2, [2, 3], 6, 0),
     ('s2', 0, 0, 3, [2, 3], 7, 0),
-    ('stt', 0, [2], [0, 1], 2, 0),
-    ('il', 'S', 2, 1, 6, 8),
+    ('stt', 0, [3], [0, 1], 3, 0),
     ('s2', 0, 1, 3, [2, 3], 7, 0),
     ('s2', 0, 2, 3, [2, 3], 7, 0),
     ('stt', 0, [2], [2, 3], 6, 0),
     ('s2', 0, 3, 3, [2, 3], 7, 0),
     ('s2', 1, 0, 0, [0, 1], 0, 0),
     ('sty', 'SP', 0, [0, 1, 2, 3], [0, 1]),
-    ('cast', 'V', 0, 2, 4),
+    ('qa', 2, 1),
     ('s2', 1, 0, 1, [0, 1], 1, 0),
-    ('cast', 'S', 0, 6, 8),
-    ('il', 'V', 3, 1, 0, 2),
     ('s2', 1, 0, 2, [0, 1], 2, 0),
     ('s2', 1, 0, 3, [0, 1], 3, 0),
+    ('cast', 'S', 0, 0, 4),
     ('s2', 1, 1, 0, [0, 1], 0, 0),
-    ('il', 'S', 3, 1, 6, 8),
-    ('qa', 2, 1),
+    ('stt', 0, [3], [2, 3], 7, 0),
     ('s2', 1, 1, 1, [0, 1], 1, 0),
     ('s2', 1, 1, 2, [0, 1], 2, 0),
     ('s2', 1, 1, 3, [0, 1], 3, 0),
-    ('stt', 0, [0], [2, 3], 4, 0),
-    ('cast', 'S', 0, 0, 2),
-    ('s2', 1, 2, 0, [0, 1], 0, 0),
     ('qa', 3, 1),
-    ('cast', 'S', 0, 4, 6),
+    ('s2', 1, 2, 0, [0, 1], 0, 0),
+    ('cast', 'S', 0, 4, 8),
+    ('sty', 'SP', 0, [0, 1, 2, 3], [2, 3]),
     ('s2', 1, 2, 1, [0, 1], 1, 0),
     ('s2', 1, 2, 2, [0, 1], 2, 0),
     ('s2', 1, 2, 3, [0, 1], 3, 0),
-    ('stt', 0, [3], [2, 3], 7, 0),
+    ('cast', 'V', 0, 12, 16),
+    ('cast', 'S', 0, 8, 12),
     ('s2', 1, 3, 0, [0, 1], 0, 0),
-    ('qy', 0, [0, 1]),
     ('s2', 1, 3, 1, [0, 1], 1, 0),
+    ('qy', 0, [0, 1]),
     ('s2', 1, 3, 2, [0, 1], 2, 0),
-    ('sty', 'SP', 0, [0, 1, 2, 3], [2, 3]),
-    ('cast', 'S', 0, 8, 10),
-    ('cast', 'V', 0, 10, 12),
     ('s2', 1, 3, 3, [0, 1], 3, 0),
+    ('stt', 1, [0], [0, 1], 0, 0),
     ('s2', 1, 0, 0, [2], 4, 0),
-    ('stt', 1, [1], [0, 1], 1, 0),
-    ('cast', 'S', 0, 14, 16),
     ('s2', 1, 1, 0, [2], 4, 0),
     ('s2', 1, 2, 0, [2], 4, 0),
     ('s2', 1, 3, 0, [2], 4, 0),
-    ('stt', 1, [2], [0, 1], 2, 0),
+    ('qy', 0, [2, 3]),
     ('s2', 1, 0, 1, [2], 5, 0),
     ('s2', 1, 1, 1, [2], 5, 0),
-    ('cast', 'S', 0, 12, 14),
     ('s2', 1, 2, 1, [2], 5, 0),
+    ('stt', 1, [2], [0, 1], 2, 0),
     ('s2', 1, 3, 1, [2], 5, 0),
-    ('stt', 1, [0], [0, 1], 0, 0),
     ('s2', 1, 0, 2, [2], 6, 0),
     ('s2', 1, 1, 2, [2], 6, 0),
     ('s2', 1, 2, 2, [2], 6, 0),
+    ('stq', 'SP', 0, [0, 1, 2, 3]),
+    ('stt', 1, [3], [0, 1], 3, 0),
     ('s2', 1, 3, 2, [2], 6, 0),
     ('s2', 1, 0, 3, [2], 7, 0),
-    ('qy', 0, [2, 3]),
     ('s2', 1, 1, 3, [2], 7, 0),
     ('s2', 1, 2, 3, [2], 7, 0),
+    ('stt', 1, [1], [0, 1], 1, 0),
     ('s2', 1, 3, 3, [2], 7, 0),
     ('s2', 1, 0, 0, [3], 0, 0),
-    ('stt', 1, [1], [2], 5, 0),
     ('s2', 1, 1, 0, [3], 0, 0),
     ('s2', 1, 2, 0, [3], 0, 0),
     ('s2', 1, 3, 0, [3], 0, 0),
-    ('stq', 'SP', 0, [0, 1, 2, 3]),
     ('stt', 1, [3], [2], 7, 0),
+    ('sty', 'SP', 1, [0, 1, 2, 3], [0, 1]),
+    ('cast', 'S', 1, 0, 4),
     ('s2', 1, 0, 1, [3], 1, 0),
+    ('stt', 1, [1], [2], 5, 0),
     ('s2', 1, 1, 1, [3], 1, 0),
-    ('stt', 1, [3], [0, 1], 3, 0),
     ('s2', 1, 2, 1, [3], 1, 0),
+    ('stt', 1, [0], [3], 0, 0),
     ('s2', 1, 3, 1, [3], 1, 0),
     ('s2', 1, 0, 2, [3], 2, 0),
-    ('s2', 1, 1, 2, [3], 2, 0),
     ('stt', 1, [0], [2], 4, 0),
+    ('s2', 1, 1, 2, [3], 2, 0),
     ('s2', 1, 2, 2, [3], 2, 0),
+    ('stt', 1, [2], [2], 6, 0),
     ('s2', 1, 3, 2, [3], 2, 0),
-    ('sty', 'SP', 1, [0, 1, 2, 3], [0, 1]),
-    ('cast', 'S', 1, 4, 6),
+    ('cast', 'S', 1, 4, 8),
     ('s2', 1, 0, 3, [3], 3, 0),
-    ('cast', 'V', 1, 0, 2),
+    ('stt', 1, [1], [3], 1, 0),
     ('s2', 1, 1, 3, [3], 3, 0),
     ('s2', 1, 2, 3, [3], 3, 0),
-    ('stt', 1, [2], [3], 2, 0),
     ('s2', 1, 3, 3, [3], 3, 0),
-    ('cast', 'S', 1, 2, 4),
-    ('stt', 1, [2], [2], 6, 0),
-    ('stt', 1, [1], [3], 1, 0),
-    ('cast', 'S', 1, 6, 8),
-    ('stt', 1, [0], [3], 0, 0),
+    ('stt', 1, [2], [3], 2, 0),
     ('sty', 'SP', 1, [0, 1, 2, 3], [2]),
-    ('stt', 1, [3], [3], 3, 0),
+    ('cast', 'V', 1, 10, 12),
     ('cast', 'S', 1, 8, 10),
+    ('stt', 1, [3], [3], 3, 0),
     ('qy', 1, [0, 1]),
-    ('cast', 'S', 1, 10, 12),
-    ('cast', 'V', 1, 12, 14),
+    ('cast', 'S', 1, 12, 14),
+    ('qy', 1, [2]),
     ('cast', 'V', 1, 14, 16),
     ('stq', 'SP', 1, [0, 1]),
     ('sty', 'SP', 1, [0, 1, 2, 3], [3]),
-    ('qy', 1, [2]),
     ('qy', 1, [3]),
     ('stq', 'SP', 1, [2, 3]),
-    ('sts', 'S', (0, 1), 2),
     ('sts', 'S', (0, 1), 0),
     ('sts', 'SP', (0, 1), 1),
+    ('sts', 'S', (0, 1), 2),
     ('sts', 'SP', (0, 1), 3),
 
 ]
@@ -334,7 +308,7 @@ def tile_newton_schulz_factor_block_h2_kernel(tc, x_words, x_scales, a4_words, a
                 nc.scalar.activation(out=prime2[:], in_=prime[:], func=ACT.Copy, scale=0.5)
             elif k == "wuq":
                 n = st[1]
-                nc.vector.memset(wu_in[:, : 4 * n], 0.0)
+                nc.vector.memset(wu_in[:, : 4 * n].bitcast(I32), 0)
                 nc.vector.quantize_mx(out=wu_codes[:, :n].bitcast(FP8X4), scales=wu_sc[:, :n], in_=wu_in[:, : 4 * n])
             elif k == "wu":
                 n = st[1]
@@ -395,8 +369,8 @@ def tile_newton_schulz_factor_block_h2_kernel(tc, x_words, x_scales, a4_words, a
                     nc.vector.tensor_scalar_mul(out=dst, in0=src, scalar1=0.5)
             elif k == "il":
                 e, G, g, m0, m1 = st[1], st[2], st[3], 16 * st[4], 16 * st[5]
-                src = a_raw[:, G, :, 512 * g + 4 * m0 : 512 * g + 4 * m1].rearrange("p j (m t) -> p m j t", t=4)
-                dst = a_il[:, G, g, :].rearrange("p (t m j) -> p m j t", t=4, j=4)[:, m0:m1, :, :]
+                src = a_raw[:, G, :, 512 * g + 4 * m0 : 512 * g + 4 * m1].rearrange("p j (m e t) -> p m t e j", t=4, e=2)
+                dst = a_il[:, G, g, :].rearrange("p (t m e j) -> p m t e j", t=4, e=2, j=4)[:, m0 // 2 : m1 // 2, :, :, :]
                 copy(e, dst, src)
             elif k == "qa":
                 G, g = st[1], st[2]

@@ -1,6 +1,7 @@
 from contextlib import ExitStack
 
 import concourse.mybir as mybir
+from concourse.masks import make_identity
 
 F32 = mybir.dt.float32
 BF16 = mybir.dt.bfloat16
@@ -15,237 +16,210 @@ ACT = mybir.ActivationFunctionType
 FLOPS = 2 * 2 * 2048 * 1024 * 512
 
 PROGRAM = [
-    ('ms', 'V', 'msw', 1024),
-    ('lda', 'SP', 0, 0, (0,)),
-    ('act0',),
-    ('lda', 'SP', 0, 1, (0,)),
-    ('lda', 'SP', 0, 2, (0,)),
-    ('lda', 'SP', 0, 3, (0,)),
     ('ms', 'V', 'msx', 256),
+    ('ms', 'V', 'msw', 1024),
     ('wuq', 128),
-    ('ldws', 'SP', 0, (0, 1, 2, 3)),
-    ('ldws', 'SP', 1, (0, 1, 2, 3)),
-    ('ldws', 'SP', 2, (0, 1, 2, 3)),
-    ('ldws', 'SP', 3, (0, 1, 2, 3)),
-    ('wu', 128, 30, 7),
-    ('ldx', 'SP'),
-    ('ldw', 'SP', (0,)),
+    ('ident',),
+    ('act0',),
+    ('wu', 128, 25, 7),
+    ('lda', 'SP', 0, (0,)),
     ('ldxs', 'SP', 0),
     ('ldxs', 'SP', 1),
-    ('il', 'V', 0, 0, 0, 4),
-    ('il', 'S', 0, 0, 4, 8),
     ('ldxs', 'SP', 2),
     ('ldxs', 'SP', 3),
+    ('ldx', 'SP'),
+    ('ldw', 'SP', (0,)),
+    ('ldws', 'SP', 0, (0, 1)),
+    ('ldws', 'SP', 1, (0, 1)),
+    ('ldws', 'SP', 2, (0, 1)),
+    ('ldws', 'SP', 3, (0, 1)),
+    ('lda', 'SP', 0, (1,)),
     ('ldw', 'SP', (1,)),
-    ('lda', 'SP', 0, 0, (1,)),
-    ('ps', (2, 3)),
-    ('ps', (0, 1)),
-    ('qa', 0, 0),
-    ('lda', 'SP', 0, 1, (1,)),
-    ('lda', 'SP', 0, 2, (1,)),
-    ('pw', 0),
-    ('lda', 'SP', 0, 3, (1,)),
-    ('lda', 'SP', 1, 0, (0, 1)),
-    ('lda', 'SP', 1, 1, (0, 1)),
-    ('lda', 'SP', 1, 2, (0, 1)),
-    ('s1', 0, 0, 0),
-    ('lda', 'SP', 1, 3, (0, 1)),
-    ('pw', 1),
+    ('lda', 'SP', 1, (0,)),
+    ('ldws', 'SP', 0, (2, 3)),
+    ('ldws', 'SP', 1, (2, 3)),
+    ('ldws', 'SP', 2, (2, 3)),
+    ('ldws', 'SP', 3, (2, 3)),
     ('ldw', 'SP', (2,)),
-    ('s1', 0, 1, 1),
-    ('ev', 'S', 0, 0, 0),
+    ('lda', 'SP', 2, (0,)),
+    ('lda', 'SP', 1, (1,)),
     ('ldw', 'SP', (3,)),
-    ('s1', 0, 2, 2),
-    ('lda', 'SP', 2, 0, (0, 1)),
-    ('ev', 'S', 0, 1, 1),
-    ('lda', 'SP', 2, 1, (0, 1)),
-    ('il', 'V', 0, 1, 0, 4),
-    ('s1', 0, 3, 3),
-    ('ev', 'S', 0, 2, 2),
-    ('lda', 'SP', 2, 2, (0, 1)),
-    ('qh', 0, [0, 1]),
-    ('s1', 1, 0, 4),
-    ('il', 'V', 0, 1, 4, 8),
-    ('ev', 'S', 0, 3, 3),
-    ('lda', 'SP', 2, 3, (0, 1)),
-    ('s1', 1, 1, 5),
-    ('lda', 'SP', 3, 0, (0, 1)),
-    ('ev', 'S', 1, 0, 4),
-    ('qh', 0, [2, 3]),
-    ('s1', 1, 2, 6),
-    ('lda', 'SP', 3, 1, (0, 1)),
-    ('il', 'V', 1, 1, 0, 4),
-    ('il', 'S', 1, 0, 0, 4),
-    ('s1', 1, 3, 7),
-    ('lda', 'SP', 3, 2, (0, 1)),
-    ('pw', 2),
-    ('il', 'V', 1, 0, 4, 8),
-    ('lda', 'SP', 3, 3, (0, 1)),
-    ('s1', 2, 0, 0),
-    ('ev', 'S', 1, 3, 7),
+    ('lda', 'SP', 3, (0,)),
+    ('lda', 'SP', 2, (1,)),
     ('ldv', 'SP', (0,)),
-    ('pw', 3),
-    ('s1', 2, 1, 1),
-    ('qa', 1, 0),
-    ('ev', 'S', 1, 2, 6),
+    ('lda', 'SP', 3, (1,)),
     ('ldv', 'SP', (1,)),
-    ('s1', 2, 2, 2),
+    ('il', 'V', 0, 0, 0, 5),
+    ('il', 'S', 0, 0, 5, 8),
+    ('qa', 0, 0),
+    ('s1', 0, 0, 0),
+    ('ev', 'S', 0, 0, 0),
+    ('s1', 0, 1, 1),
+    ('ev', 'S', 0, 1, 1),
+    ('s1', 0, 2, 2),
+    ('ev', 'S', 0, 2, 2),
+    ('s1', 0, 3, 3),
+    ('ev', 'S', 0, 3, 3),
+    ('il', 'V', 0, 1, 0, 8),
+    ('il', 'V', 1, 0, 0, 8),
     ('qa', 0, 1),
-    ('ev', 'S', 1, 1, 5),
-    ('qh', 1, [2, 3]),
-    ('ev', 'S', 2, 1, 1),
-    ('s1', 2, 3, 3),
-    ('il', 'V', 2, 0, 4, 8),
-    ('ev', 'S', 2, 2, 2),
-    ('s1', 3, 0, 4),
-    ('qh', 1, [0, 1]),
-    ('ev', 'S', 2, 3, 3),
-    ('il', 'V', 2, 0, 0, 4),
-    ('s1', 3, 1, 5),
-    ('ev', 'S', 2, 0, 0),
-    ('s1', 3, 2, 6),
-    ('qh', 2, [2, 3]),
-    ('ev', 'S', 3, 1, 5),
+    ('qa', 1, 0),
+    ('s1', 1, 0, 0),
+    ('ev', 'S', 1, 0, 0),
+    ('s1', 1, 1, 1),
+    ('ev', 'S', 1, 1, 1),
+    ('s1', 1, 2, 2),
+    ('ev', 'S', 1, 2, 2),
+    ('s1', 1, 3, 3),
+    ('ev', 'S', 1, 3, 3),
+    ('tr', 0, 0, 4, 1),
+    ('tr', 0, 1, 5, 1),
+    ('cp', 'S', 0, 0, 4),
+    ('cp', 'S', 0, 1, 5),
+    ('il', 'V', 2, 0, 0, 8),
+    ('qh', 0, [0, 1, 2, 3]),
     ('qa', 2, 0),
-    ('s1', 3, 3, 7),
-    ('il', 'S', 3, 0, 4, 8),
-    ('qh', 2, [0, 1]),
-    ('il', 'V', 3, 0, 0, 4),
-    ('s2', 0, 0, 0, [0, 1], 0, 0),
-    ('s2', 0, 0, 1, [0, 1], 1, 0),
-    ('s2', 0, 0, 2, [0, 1], 2, 0),
-    ('s2', 0, 0, 3, [0, 1], 3, 0),
-    ('s2', 0, 1, 0, [0, 1], 0, 0),
-    ('il', 'V', 1, 1, 4, 8),
-    ('s2', 0, 1, 1, [0, 1], 1, 0),
-    ('ev', 'S', 3, 3, 7),
-    ('s2', 0, 1, 2, [0, 1], 2, 0),
-    ('s2', 0, 1, 3, [0, 1], 3, 0),
-    ('s2', 0, 2, 0, [0, 1], 0, 0),
-    ('s2', 0, 2, 1, [0, 1], 1, 0),
+    ('s1', 2, 0, 0),
+    ('ev', 'S', 2, 0, 0),
+    ('s1', 2, 1, 1),
+    ('ev', 'S', 2, 1, 1),
+    ('s1', 2, 2, 2),
+    ('ev', 'S', 2, 2, 2),
+    ('s1', 2, 3, 3),
+    ('ev', 'S', 2, 3, 3),
+    ('tr', 1, 0, 6, 1),
+    ('tr', 1, 1, 7, 1),
+    ('cp', 'S', 1, 0, 6),
+    ('cp', 'S', 1, 1, 7),
+    ('il', 'V', 1, 1, 0, 8),
+    ('il', 'V', 3, 0, 0, 8),
+    ('qh', 1, [0, 1, 2, 3]),
     ('qa', 3, 0),
-    ('ev', 'S', 3, 0, 4),
-    ('s2', 0, 2, 2, [0, 1], 2, 0),
-    ('s2', 0, 2, 3, [0, 1], 3, 0),
     ('qa', 1, 1),
-    ('ev', 'S', 3, 2, 6),
+    ('s1', 3, 0, 0),
+    ('ev', 'S', 3, 0, 0),
+    ('s1', 3, 1, 1),
+    ('ev', 'S', 3, 1, 1),
+    ('s1', 3, 2, 2),
+    ('ev', 'S', 3, 2, 2),
+    ('s1', 3, 3, 3),
+    ('ev', 'S', 3, 3, 3),
+    ('tr', 2, 0, 4, 1),
+    ('tr', 2, 1, 5, 1),
+    ('cp', 'S', 2, 0, 4),
+    ('cp', 'S', 2, 1, 5),
+    ('il', 'V', 2, 1, 0, 6),
+    ('qh', 2, [0, 1, 2, 3]),
+    ('s2', 0, 0, 0, [0, 1, 2, 3], 0, 0),
+    ('s2', 0, 0, 1, [0, 1, 2, 3], 1, 0),
+    ('tr', 3, 0, 6, 1),
+    ('tr', 3, 1, 7, 1),
+    ('cp', 'S', 3, 0, 6),
+    ('cp', 'S', 3, 1, 7),
+    ('s2', 0, 0, 2, [0, 1, 2, 3], 2, 0),
+    ('s2', 0, 0, 3, [0, 1, 2, 3], 3, 0),
     ('qh', 3, [0, 1]),
-    ('il', 'S', 2, 1, 4, 8),
+    ('il', 'S', 2, 1, 6, 8),
+    ('il', 'S', 3, 1, 0, 8),
     ('qh', 3, [2, 3]),
-    ('s2', 0, 3, 0, [0, 1], 0, 0),
-    ('il', 'V', 2, 1, 0, 4),
-    ('s2', 0, 3, 1, [0, 1], 1, 0),
-    ('s2', 0, 3, 2, [0, 1], 2, 0),
-    ('s2', 0, 3, 3, [0, 1], 3, 0),
-    ('s2', 0, 0, 0, [2, 3], 4, 0),
-    ('s2', 0, 1, 0, [2, 3], 4, 0),
-    ('stt', 0, [1], [0, 1], 1, 0),
-    ('il', 'S', 3, 1, 0, 4),
-    ('s2', 0, 2, 0, [2, 3], 4, 0),
-    ('s2', 0, 3, 0, [2, 3], 4, 0),
-    ('stt', 0, [2], [0, 1], 2, 0),
-    ('s2', 0, 0, 1, [2, 3], 5, 0),
-    ('s2', 0, 1, 1, [2, 3], 5, 0),
-    ('stt', 0, [0], [0, 1], 0, 0),
-    ('s2', 0, 2, 1, [2, 3], 5, 0),
-    ('s2', 0, 3, 1, [2, 3], 5, 0),
-    ('s2', 0, 0, 2, [2, 3], 6, 0),
-    ('stt', 0, [0], [2, 3], 4, 0),
-    ('s2', 0, 1, 2, [2, 3], 6, 0),
-    ('s2', 0, 2, 2, [2, 3], 6, 0),
-    ('stt', 0, [1], [2, 3], 5, 0),
-    ('il', 'S', 3, 1, 4, 8),
-    ('s2', 0, 3, 2, [2, 3], 6, 0),
-    ('s2', 0, 0, 3, [2, 3], 7, 0),
-    ('stt', 0, [3], [0, 1], 3, 0),
-    ('s2', 0, 1, 3, [2, 3], 7, 0),
-    ('s2', 0, 2, 3, [2, 3], 7, 0),
-    ('stt', 0, [2], [2, 3], 6, 0),
-    ('s2', 0, 3, 3, [2, 3], 7, 0),
-    ('s2', 1, 0, 0, [0, 1], 0, 0),
-    ('sty', 'SP', 0, [0, 1, 2, 3], [0, 1]),
     ('qa', 2, 1),
-    ('s2', 1, 0, 1, [0, 1], 1, 0),
-    ('s2', 1, 0, 2, [0, 1], 2, 0),
-    ('s2', 1, 0, 3, [0, 1], 3, 0),
-    ('cast', 'S', 0, 0, 4),
-    ('s2', 1, 1, 0, [0, 1], 0, 0),
-    ('stt', 0, [3], [2, 3], 7, 0),
-    ('s2', 1, 1, 1, [0, 1], 1, 0),
-    ('s2', 1, 1, 2, [0, 1], 2, 0),
-    ('s2', 1, 1, 3, [0, 1], 3, 0),
+    ('s2', 0, 1, 0, [0, 1, 2, 3], 0, 0),
+    ('s2', 0, 1, 1, [0, 1, 2, 3], 1, 0),
+    ('s2', 0, 1, 2, [0, 1, 2, 3], 2, 0),
+    ('s2', 0, 1, 3, [0, 1, 2, 3], 3, 0),
+    ('s2', 0, 2, 0, [0, 1, 2, 3], 0, 0),
+    ('s2', 0, 2, 1, [0, 1, 2, 3], 1, 0),
+    ('s2', 0, 2, 2, [0, 1, 2, 3], 2, 0),
+    ('s2', 0, 2, 3, [0, 1, 2, 3], 3, 0),
+    ('s2', 0, 3, 0, [0, 1, 2, 3], 0, 0),
+    ('s2', 0, 3, 1, [0, 1, 2, 3], 1, 0),
+    ('s2', 0, 3, 2, [0, 1, 2, 3], 2, 0),
+    ('s2', 0, 3, 3, [0, 1, 2, 3], 3, 0),
+    ('s2', 1, 0, 0, [0, 1], 4, 0),
+    ('s2', 1, 0, 1, [0, 1], 5, 0),
+    ('s2', 1, 0, 2, [0, 1], 6, 0),
+    ('s2', 1, 0, 3, [0, 1], 7, 0),
+    ('s2', 1, 1, 0, [0, 1], 4, 0),
+    ('s2', 1, 1, 1, [0, 1], 5, 0),
+    ('s2', 1, 1, 2, [0, 1], 6, 0),
+    ('s2', 1, 1, 3, [0, 1], 7, 0),
+    ('s2', 1, 2, 0, [0, 1], 4, 0),
+    ('s2', 1, 2, 1, [0, 1], 5, 0),
+    ('s2', 1, 2, 2, [0, 1], 6, 0),
+    ('s2', 1, 2, 3, [0, 1], 7, 0),
+    ('stt', 0, [0], [0, 1], 0, 0),
+    ('stt', 0, [1], [0, 1], 1, 0),
+    ('stt', 0, [2], [0, 1], 2, 0),
+    ('stt', 0, [3], [0, 1], 3, 0),
+    ('sty', 'SP', 0, [0, 1, 2, 3], [0, 1]),
+    ('cast', 'S', 0, 0, 8),
+    ('stt', 0, [0], [2, 3], 0, 256),
+    ('stt', 0, [1], [2, 3], 1, 256),
     ('qa', 3, 1),
-    ('s2', 1, 2, 0, [0, 1], 0, 0),
-    ('cast', 'S', 0, 4, 8),
+    ('stt', 0, [2], [2, 3], 2, 256),
+    ('stt', 0, [3], [2, 3], 3, 256),
     ('sty', 'SP', 0, [0, 1, 2, 3], [2, 3]),
-    ('s2', 1, 2, 1, [0, 1], 1, 0),
-    ('s2', 1, 2, 2, [0, 1], 2, 0),
-    ('s2', 1, 2, 3, [0, 1], 3, 0),
-    ('cast', 'V', 0, 12, 16),
-    ('cast', 'S', 0, 8, 12),
-    ('s2', 1, 3, 0, [0, 1], 0, 0),
-    ('s2', 1, 3, 1, [0, 1], 1, 0),
+    ('cast', 'S', 0, 8, 16),
     ('qy', 0, [0, 1]),
-    ('s2', 1, 3, 2, [0, 1], 2, 0),
-    ('s2', 1, 3, 3, [0, 1], 3, 0),
-    ('stt', 1, [0], [0, 1], 0, 0),
-    ('s2', 1, 0, 0, [2], 4, 0),
-    ('s2', 1, 1, 0, [2], 4, 0),
-    ('s2', 1, 2, 0, [2], 4, 0),
-    ('s2', 1, 3, 0, [2], 4, 0),
-    ('qy', 0, [2, 3]),
-    ('s2', 1, 0, 1, [2], 5, 0),
-    ('s2', 1, 1, 1, [2], 5, 0),
-    ('s2', 1, 2, 1, [2], 5, 0),
-    ('stt', 1, [2], [0, 1], 2, 0),
-    ('s2', 1, 3, 1, [2], 5, 0),
-    ('s2', 1, 0, 2, [2], 6, 0),
-    ('s2', 1, 1, 2, [2], 6, 0),
-    ('s2', 1, 2, 2, [2], 6, 0),
-    ('stq', 'SP', 0, [0, 1, 2, 3]),
-    ('stt', 1, [3], [0, 1], 3, 0),
-    ('s2', 1, 3, 2, [2], 6, 0),
-    ('s2', 1, 0, 3, [2], 7, 0),
-    ('s2', 1, 1, 3, [2], 7, 0),
-    ('s2', 1, 2, 3, [2], 7, 0),
-    ('stt', 1, [1], [0, 1], 1, 0),
-    ('s2', 1, 3, 3, [2], 7, 0),
-    ('s2', 1, 0, 0, [3], 0, 0),
-    ('s2', 1, 1, 0, [3], 0, 0),
-    ('s2', 1, 2, 0, [3], 0, 0),
-    ('s2', 1, 3, 0, [3], 0, 0),
-    ('stt', 1, [3], [2], 7, 0),
+    ('s2', 1, 3, 0, [0, 1], 4, 0),
+    ('s2', 1, 3, 1, [0, 1], 5, 0),
+    ('s2', 1, 3, 2, [0, 1], 6, 0),
+    ('s2', 1, 3, 3, [0, 1], 7, 0),
+    ('stt', 1, [0], [0, 1], 4, 0),
+    ('stt', 1, [1], [0, 1], 5, 0),
+    ('stt', 1, [2], [0, 1], 6, 0),
+    ('stt', 1, [3], [0, 1], 7, 0),
     ('sty', 'SP', 1, [0, 1, 2, 3], [0, 1]),
-    ('cast', 'S', 1, 0, 4),
-    ('s2', 1, 0, 1, [3], 1, 0),
-    ('stt', 1, [1], [2], 5, 0),
-    ('s2', 1, 1, 1, [3], 1, 0),
-    ('s2', 1, 2, 1, [3], 1, 0),
-    ('stt', 1, [0], [3], 0, 0),
-    ('s2', 1, 3, 1, [3], 1, 0),
-    ('s2', 1, 0, 2, [3], 2, 0),
-    ('stt', 1, [0], [2], 4, 0),
-    ('s2', 1, 1, 2, [3], 2, 0),
-    ('s2', 1, 2, 2, [3], 2, 0),
-    ('stt', 1, [2], [2], 6, 0),
-    ('s2', 1, 3, 2, [3], 2, 0),
-    ('cast', 'S', 1, 4, 8),
-    ('s2', 1, 0, 3, [3], 3, 0),
-    ('stt', 1, [1], [3], 1, 0),
-    ('s2', 1, 1, 3, [3], 3, 0),
-    ('s2', 1, 2, 3, [3], 3, 0),
-    ('s2', 1, 3, 3, [3], 3, 0),
-    ('stt', 1, [2], [3], 2, 0),
+    ('qy', 0, [2, 3]),
+    ('stq', 'SP', 0, [0, 1, 2, 3]),
+    ('cast', 'S', 1, 0, 8),
+    ('s2', 1, 0, 0, [2], 0, 0),
+    ('s2', 1, 1, 0, [2], 0, 0),
+    ('s2', 1, 2, 0, [2], 0, 0),
+    ('s2', 1, 3, 0, [2], 0, 0),
+    ('s2', 1, 0, 1, [2], 1, 0),
+    ('s2', 1, 1, 1, [2], 1, 0),
+    ('s2', 1, 2, 1, [2], 1, 0),
+    ('s2', 1, 3, 1, [2], 1, 0),
+    ('s2', 1, 0, 2, [2], 2, 0),
+    ('s2', 1, 1, 2, [2], 2, 0),
+    ('s2', 1, 2, 2, [2], 2, 0),
+    ('s2', 1, 3, 2, [2], 2, 0),
+    ('s2', 1, 0, 3, [2], 3, 0),
+    ('s2', 1, 1, 3, [2], 3, 0),
+    ('s2', 1, 2, 3, [2], 3, 0),
+    ('s2', 1, 3, 3, [2], 3, 0),
+    ('stt', 1, [0], [2], 0, 0),
+    ('stt', 1, [1], [2], 1, 0),
+    ('stt', 1, [2], [2], 2, 0),
+    ('stt', 1, [3], [2], 3, 0),
     ('sty', 'SP', 1, [0, 1, 2, 3], [2]),
-    ('cast', 'V', 1, 10, 12),
-    ('cast', 'S', 1, 8, 10),
-    ('stt', 1, [3], [3], 3, 0),
-    ('qy', 1, [0, 1]),
-    ('cast', 'S', 1, 12, 14),
-    ('qy', 1, [2]),
-    ('cast', 'V', 1, 14, 16),
-    ('stq', 'SP', 1, [0, 1]),
+    ('cast', 'S', 1, 8, 12),
+    ('s2', 1, 0, 0, [3], 4, 0),
+    ('s2', 1, 1, 0, [3], 4, 0),
+    ('s2', 1, 2, 0, [3], 4, 0),
+    ('s2', 1, 3, 0, [3], 4, 0),
+    ('s2', 1, 0, 1, [3], 5, 0),
+    ('s2', 1, 1, 1, [3], 5, 0),
+    ('s2', 1, 2, 1, [3], 5, 0),
+    ('s2', 1, 3, 1, [3], 5, 0),
+    ('s2', 1, 0, 2, [3], 6, 0),
+    ('s2', 1, 1, 2, [3], 6, 0),
+    ('s2', 1, 2, 2, [3], 6, 0),
+    ('s2', 1, 3, 2, [3], 6, 0),
+    ('s2', 1, 0, 3, [3], 7, 0),
+    ('s2', 1, 1, 3, [3], 7, 0),
+    ('s2', 1, 2, 3, [3], 7, 0),
+    ('s2', 1, 3, 3, [3], 7, 0),
+    ('stt', 1, [0], [3], 4, 0),
+    ('stt', 1, [1], [3], 5, 0),
+    ('stt', 1, [2], [3], 6, 0),
+    ('stt', 1, [3], [3], 7, 0),
     ('sty', 'SP', 1, [0, 1, 2, 3], [3]),
+    ('qy', 1, [0, 1]),
+    ('stq', 'SP', 1, [0, 1]),
+    ('cast', 'V', 1, 12, 16),
+    ('qy', 1, [2]),
     ('qy', 1, [3]),
     ('stq', 'SP', 1, [2, 3]),
     ('sts', 'S', (0, 1), 0),
@@ -264,10 +238,10 @@ def tile_newton_schulz_factor_block_h2_kernel(tc, x_words, x_scales, a4_words, a
         ps = ctx.enter_context(tc.psum_pool(name="ps", bufs=1))
         x_codes = sb.tile([128, 2, 512], U32, align_bytes=256)
         x_sc = sb.tile([128, 2, 512], U8, align_bytes=256)
-        w_raw = sb.tile([128, 4, 2, 1024], U8, align_bytes=256)
-        w_perm = sb.tile([128, 4, 4, 2, 256], U8, align_bytes=256)
+        w_codes = sb.tile([128, 2, 4096], U8, align_bytes=256)
+        h_t = sb.tile([128, 4, 4, 512], BF16, align_bytes=256)
+        ident = sb.tile([128, 128], F32, align_bytes=256)
         ws_raw = sb.tile([128, 2, 2048], U8, align_bytes=256)
-        ws_perm = sb.tile([128, 2, 4, 4, 128], U8, align_bytes=256)
         a_raw = sb.tile([128, 4, 4, 1024], BF16, align_bytes=256)
         a_il = sb.tile([128, 4, 2, 2048], BF16, align_bytes=256)
         a_codes = sb.tile([128, 4, 2, 512], U32, align_bytes=256)
@@ -329,44 +303,47 @@ def tile_newton_schulz_factor_block_h2_kernel(tc, x_words, x_scales, a4_words, a
                                      in_=a4_scales.rearrange("g (q r) n -> r q g n", r=4)[r][:, :, cols].bitcast(I32))
             elif k == "ldw":
                 for G in st[2]:
-                    eng[st[1]].dma_start(out=w_raw[:, G, :, :].bitcast(I32),
+                    eng[st[1]].dma_start(out=w_codes[:, :, 1024 * G : 1024 * (G + 1)].bitcast(I32),
                                          in_=a4_words[:, :, 1024 * G : 1024 * (G + 1)].rearrange("g p n -> p g n").bitcast(I32))
             elif k == "lda":
-                G, t, gs = st[2], st[3], st[4]
+                G, gs = st[2], st[3]
                 cols = slice(512 * gs[0], 512 * (gs[-1] + 1))
-                rows = a[512 * G : 512 * (G + 1), :].rearrange("(j t i) q -> t j i q", t=4, i=8)
-                eng[st[1]].dma_start(out=a_raw[:, G, t, cols], in_=rows[t][:, :, cols])
+                rows = a[512 * G : 512 * (G + 1), :].rearrange("(p j) q -> p j q", j=4)
+                eng[st[1]].dma_start(out=a_raw[:, G, :, cols], in_=rows[:, :, cols])
+            elif k == "ident":
+                make_identity(nc, ident[:])
             elif k == "ldv":
                 for g in st[2]:
                     eng[st[1]].dma_start(out=v_sb[:, g, :, :], in_=v[512 * g : 512 * (g + 1), :].rearrange("(p t) m -> p t m", t=4))
-            elif k == "pw":
-                G = st[1]
-                src = w_raw[:, G, :, :].rearrange("p g n -> p (g n)").bitcast(I32).rearrange("p (j t i) -> p t j i", t=4, i=4)
-                dst = w_perm[:, G, :, :, :].rearrange("p t g n -> p (t g n)").bitcast(I32).rearrange("p (t j i) -> p t j i", t=4, i=4)
-                nc.vector.tensor_copy(out=dst, in_=src)
-            elif k == "ps":
-                G0, G1 = st[1][0], st[1][-1] + 1
-                for gk in range(2):
-                    src = ws_raw[:, gk, 512 * G0 : 512 * G1].bitcast(I32).rearrange("p (j t i) -> p t j i", t=4, i=2)
-                    dst = ws_perm[:, gk, :, G0:G1, :].rearrange("p t G n -> p t (G n)").bitcast(I32).rearrange("p t (j i) -> p t j i", i=2)
-                    nc.vector.tensor_copy(out=dst, in_=src)
             elif k == "s1":
                 G, c = st[1], st[2]
                 bank = new_bank(st[3])
-                for t in range(4):
-                    for gk in range(2):
-                        nc.tensor.matmul_mx(out=bank[:, 128 * t : 128 * (t + 1)],
-                                            lhsT=w_perm[:, G, t, gk, :].bitcast(FP4X4), lhsT_scale=ws_perm[:, gk, t, G, :],
-                                            rhs=x_codes[:, gk, 128 * c : 128 * (c + 1)].bitcast(FP8X4),
-                                            rhs_scale=x_sc[:, gk, 128 * c : 128 * (c + 1)], start=(gk == 0), stop=(gk == 1))
+                for gk in range(2):
+                    nc.tensor.matmul_mx(out=bank[:],
+                                        lhsT=x_codes[:, gk, 128 * c : 128 * (c + 1)].bitcast(FP8X4), lhsT_scale=x_sc[:, gk, 128 * c : 128 * (c + 1)],
+                                        rhs=w_codes[:, gk, 1024 * G : 1024 * (G + 1)].bitcast(FP4X4),
+                                        rhs_scale=ws_raw[:, gk, 512 * G : 512 * (G + 1)], start=(gk == 0), stop=(gk == 1))
             elif k == "ev":
                 e, G, c = st[1], st[2], st[3]
-                src = banks[st[4]][:].rearrange("p (t m) -> p m t", t=4)
-                dst = h_il[:, G, 512 * c : 512 * (c + 1)].rearrange("p (m t) -> p m t", t=4)
+                src = banks[st[4]][:].rearrange("m (p u e) -> m u p e", u=2, e=2)
+                dst = h_t[:, G, c, :].rearrange("m (u p e) -> m u p e", u=2, e=2)
                 if e == "S":
                     nc.scalar.activation(out=dst, in_=src, func=ACT.Copy, scale=0.5)
                 else:
                     nc.vector.tensor_scalar_mul(out=dst, in0=src, scalar1=0.5)
+            elif k == "tr":
+                G, h = st[1], st[2]
+                bank = new_bank(st[3])
+                for cc in range(2):
+                    words = h_t[:, G, 2 * h + cc, :].bitcast(F32)
+                    for u in range(2):
+                        i = 2 * cc + u
+                        nc.tensor.transpose(bank[:, 128 * i : 128 * (i + 1)], words[:, 128 * u : 128 * (u + 1)], ident[:])
+            elif k == "cp":
+                e, G, h = st[1], st[2], st[3]
+                src = banks[st[4]][:].rearrange("p (c u m) -> p c m u", c=2, u=2)
+                dst = h_il[:, G, 1024 * h : 1024 * (h + 1)].bitcast(F32).rearrange("p (c m u) -> p c m u", c=2, u=2)
+                copy(e, dst, src)
             elif k == "il":
                 e, G, g, m0, m1 = st[1], st[2], st[3], 16 * st[4], 16 * st[5]
                 src = a_raw[:, G, :, 512 * g + 4 * m0 : 512 * g + 4 * m1].rearrange("p j (m e t) -> p m t e j", t=4, e=2)

@@ -16,209 +16,227 @@ ACT = mybir.ActivationFunctionType
 FLOPS = 2 * 2 * 2048 * 1024 * 512
 
 PROGRAM = [
-    ('ms', 'V', 'msx', 256),
-    ('ms', 'V', 'msw', 1024),
-    ('wuq', 128),
+    ('ms', 'G', 'msx', 256),
     ('ident',),
-    ('act0',),
-    ('wu', 128, 25, 7),
-    ('lda', 'SP', 0, (0,)),
+    ('ms', 'V', 'msw0', 512),
     ('ldxs', 'SP', 0),
+    ('act0',),
     ('ldxs', 'SP', 1),
     ('ldxs', 'SP', 2),
     ('ldxs', 'SP', 3),
-    ('ldx', 'SP'),
+    ('wuq', 128),
+    ('lda', 'SP', 0, (0,)),
+    ('ldx', 'SP', 0),
     ('ldw', 'SP', (0,)),
     ('ldws', 'SP', 0, (0, 1)),
+    ('ms', 'V', 'msw1', 512),
+    ('wu', 128, 25, 7),
     ('ldws', 'SP', 1, (0, 1)),
     ('ldws', 'SP', 2, (0, 1)),
     ('ldws', 'SP', 3, (0, 1)),
+    ('ldx', 'SP', 1),
     ('lda', 'SP', 0, (1,)),
+    ('il', 'V', 0, 0, 0, 6),
+    ('il', 'S', 0, 0, 6, 8),
     ('ldw', 'SP', (1,)),
     ('lda', 'SP', 1, (0,)),
     ('ldws', 'SP', 0, (2, 3)),
+    ('qa', 0, 0),
     ('ldws', 'SP', 1, (2, 3)),
     ('ldws', 'SP', 2, (2, 3)),
     ('ldws', 'SP', 3, (2, 3)),
+    ('s1', 0, 0, 0),
     ('ldw', 'SP', (2,)),
+    ('s1', 0, 1, 1),
+    ('ev', 'S', 0, 0, 0),
+    ('s1', 0, 2, 2),
+    ('ev', 'S', 0, 1, 1),
     ('lda', 'SP', 2, (0,)),
+    ('il', 'V', 0, 1, 0, 8),
+    ('s1', 0, 3, 3),
+    ('ev', 'S', 0, 2, 2),
     ('lda', 'SP', 1, (1,)),
+    ('s1', 1, 0, 0),
+    ('ev', 'S', 0, 3, 3),
+    ('s1', 1, 1, 1),
+    ('ev', 'S', 1, 0, 0),
     ('ldw', 'SP', (3,)),
+    ('il', 'V', 1, 0, 0, 8),
+    ('s1', 1, 2, 2),
     ('lda', 'SP', 3, (0,)),
     ('lda', 'SP', 2, (1,)),
-    ('ldv', 'SP', (0,)),
-    ('lda', 'SP', 3, (1,)),
-    ('ldv', 'SP', (1,)),
-    ('il', 'V', 0, 0, 0, 5),
-    ('il', 'S', 0, 0, 5, 8),
-    ('qa', 0, 0),
-    ('s1', 0, 0, 0),
-    ('ev', 'S', 0, 0, 0),
-    ('s1', 0, 1, 1),
-    ('ev', 'S', 0, 1, 1),
-    ('s1', 0, 2, 2),
-    ('ev', 'S', 0, 2, 2),
-    ('s1', 0, 3, 3),
-    ('ev', 'S', 0, 3, 3),
-    ('il', 'V', 0, 1, 0, 8),
-    ('il', 'V', 1, 0, 0, 8),
-    ('qa', 0, 1),
-    ('qa', 1, 0),
-    ('s1', 1, 0, 0),
-    ('ev', 'S', 1, 0, 0),
-    ('s1', 1, 1, 1),
     ('ev', 'S', 1, 1, 1),
-    ('s1', 1, 2, 2),
-    ('ev', 'S', 1, 2, 2),
+    ('ldv', 'SP', (0,)),
     ('s1', 1, 3, 3),
-    ('ev', 'S', 1, 3, 3),
+    ('lda', 'SP', 3, (1,)),
+    ('ev', 'S', 1, 2, 2),
     ('tr', 0, 0, 4, 1),
+    ('ldv', 'SP', (1,)),
+    ('qa', 0, 1),
+    ('ev', 'S', 1, 3, 3),
     ('tr', 0, 1, 5, 1),
-    ('cp', 'S', 0, 0, 4),
-    ('cp', 'S', 0, 1, 5),
-    ('il', 'V', 2, 0, 0, 8),
-    ('qh', 0, [0, 1, 2, 3]),
-    ('qa', 2, 0),
+    ('qa', 1, 0),
     ('s1', 2, 0, 0),
-    ('ev', 'S', 2, 0, 0),
+    ('cp', 'S', 0, 0, 4),
+    ('il', 'V', 2, 0, 0, 8),
     ('s1', 2, 1, 1),
-    ('ev', 'S', 2, 1, 1),
+    ('cp', 'S', 0, 1, 5),
     ('s1', 2, 2, 2),
-    ('ev', 'S', 2, 2, 2),
+    ('ev', 'S', 2, 0, 0),
     ('s1', 2, 3, 3),
-    ('ev', 'S', 2, 3, 3),
+    ('ev', 'S', 2, 1, 1),
+    ('qh', 0, [0, 1, 2, 3]),
     ('tr', 1, 0, 6, 1),
+    ('ev', 'S', 2, 2, 2),
+    ('qa', 2, 0),
     ('tr', 1, 1, 7, 1),
-    ('cp', 'S', 1, 0, 6),
-    ('cp', 'S', 1, 1, 7),
+    ('ev', 'S', 2, 3, 3),
     ('il', 'V', 1, 1, 0, 8),
-    ('il', 'V', 3, 0, 0, 8),
-    ('qh', 1, [0, 1, 2, 3]),
-    ('qa', 3, 0),
-    ('qa', 1, 1),
     ('s1', 3, 0, 0),
-    ('ev', 'S', 3, 0, 0),
+    ('cp', 'S', 1, 0, 6),
     ('s1', 3, 1, 1),
-    ('ev', 'S', 3, 1, 1),
+    ('cp', 'S', 1, 1, 7),
     ('s1', 3, 2, 2),
-    ('ev', 'S', 3, 2, 2),
+    ('il', 'V', 3, 0, 0, 8),
+    ('ev', 'S', 3, 0, 0),
     ('s1', 3, 3, 3),
-    ('ev', 'S', 3, 3, 3),
+    ('ev', 'S', 3, 1, 1),
     ('tr', 2, 0, 4, 1),
+    ('ev', 'S', 3, 2, 2),
+    ('qh', 1, [0, 1, 2, 3]),
     ('tr', 2, 1, 5, 1),
+    ('s2', 0, 0, 0, [0, 1], 0, 0),
+    ('ev', 'S', 3, 3, 3),
+    ('qa', 3, 0),
+    ('s2', 0, 0, 1, [0, 1], 1, 0),
+    ('s2', 0, 0, 2, [0, 1], 2, 0),
+    ('s2', 0, 1, 0, [0, 1], 0, 0),
+    ('s2', 0, 1, 1, [0, 1], 1, 0),
     ('cp', 'S', 2, 0, 4),
-    ('cp', 'S', 2, 1, 5),
     ('il', 'V', 2, 1, 0, 6),
-    ('qh', 2, [0, 1, 2, 3]),
-    ('s2', 0, 0, 0, [0, 1, 2, 3], 0, 0),
-    ('s2', 0, 0, 1, [0, 1, 2, 3], 1, 0),
+    ('s2', 0, 1, 2, [0, 1], 2, 0),
     ('tr', 3, 0, 6, 1),
+    ('cp', 'S', 2, 1, 5),
     ('tr', 3, 1, 7, 1),
     ('cp', 'S', 3, 0, 6),
+    ('s2', 0, 0, 3, [0, 1], 3, 0),
+    ('s2', 0, 1, 3, [0, 1], 3, 0),
+    ('qh', 2, [0, 1, 2, 3]),
+    ('s2', 0, 0, 0, [2, 3], 4, 0),
+    ('s2', 0, 0, 1, [2, 3], 5, 0),
     ('cp', 'S', 3, 1, 7),
-    ('s2', 0, 0, 2, [0, 1, 2, 3], 2, 0),
-    ('s2', 0, 0, 3, [0, 1, 2, 3], 3, 0),
-    ('qh', 3, [0, 1]),
+    ('s2', 0, 1, 0, [2, 3], 4, 0),
+    ('s2', 0, 1, 1, [2, 3], 5, 0),
+    ('qa', 1, 1),
+    ('s2', 0, 2, 0, [0, 1], 0, 0),
     ('il', 'S', 2, 1, 6, 8),
-    ('il', 'S', 3, 1, 0, 8),
+    ('s2', 0, 2, 1, [0, 1], 1, 0),
+    ('s2', 0, 2, 2, [0, 1], 2, 0),
+    ('qh', 3, [0, 1]),
+    ('s2', 0, 2, 3, [0, 1], 3, 0),
+    ('s2', 0, 0, 2, [2, 3], 6, 0),
     ('qh', 3, [2, 3]),
+    ('s2', 0, 0, 3, [2, 3], 7, 0),
+    ('il', 'S', 3, 1, 0, 8),
+    ('s2', 0, 1, 2, [2, 3], 6, 0),
     ('qa', 2, 1),
-    ('s2', 0, 1, 0, [0, 1, 2, 3], 0, 0),
-    ('s2', 0, 1, 1, [0, 1, 2, 3], 1, 0),
-    ('s2', 0, 1, 2, [0, 1, 2, 3], 2, 0),
-    ('s2', 0, 1, 3, [0, 1, 2, 3], 3, 0),
-    ('s2', 0, 2, 0, [0, 1, 2, 3], 0, 0),
-    ('s2', 0, 2, 1, [0, 1, 2, 3], 1, 0),
-    ('s2', 0, 2, 2, [0, 1, 2, 3], 2, 0),
-    ('s2', 0, 2, 3, [0, 1, 2, 3], 3, 0),
-    ('s2', 0, 3, 0, [0, 1, 2, 3], 0, 0),
-    ('s2', 0, 3, 1, [0, 1, 2, 3], 1, 0),
-    ('s2', 0, 3, 2, [0, 1, 2, 3], 2, 0),
-    ('s2', 0, 3, 3, [0, 1, 2, 3], 3, 0),
-    ('s2', 1, 0, 0, [0, 1], 4, 0),
-    ('s2', 1, 0, 1, [0, 1], 5, 0),
-    ('s2', 1, 0, 2, [0, 1], 6, 0),
-    ('s2', 1, 0, 3, [0, 1], 7, 0),
-    ('s2', 1, 1, 0, [0, 1], 4, 0),
-    ('s2', 1, 1, 1, [0, 1], 5, 0),
-    ('s2', 1, 1, 2, [0, 1], 6, 0),
-    ('s2', 1, 1, 3, [0, 1], 7, 0),
-    ('s2', 1, 2, 0, [0, 1], 4, 0),
-    ('s2', 1, 2, 1, [0, 1], 5, 0),
-    ('s2', 1, 2, 2, [0, 1], 6, 0),
-    ('s2', 1, 2, 3, [0, 1], 7, 0),
+    ('s2', 0, 1, 3, [2, 3], 7, 0),
+    ('s2', 0, 3, 0, [0, 1], 0, 0),
+    ('s2', 0, 3, 1, [0, 1], 1, 0),
+    ('s2', 0, 3, 2, [0, 1], 2, 0),
+    ('s2', 0, 3, 3, [0, 1], 3, 0),
     ('stt', 0, [0], [0, 1], 0, 0),
+    ('s2', 0, 2, 0, [2, 3], 4, 0),
+    ('s2', 0, 2, 1, [2, 3], 5, 0),
     ('stt', 0, [1], [0, 1], 1, 0),
+    ('s2', 0, 2, 2, [2, 3], 6, 0),
+    ('s2', 0, 2, 3, [2, 3], 7, 0),
     ('stt', 0, [2], [0, 1], 2, 0),
+    ('s2', 0, 3, 0, [2, 3], 4, 0),
+    ('s2', 0, 3, 1, [2, 3], 5, 0),
     ('stt', 0, [3], [0, 1], 3, 0),
+    ('s2', 0, 3, 2, [2, 3], 6, 0),
+    ('s2', 0, 3, 3, [2, 3], 7, 0),
+    ('stt', 0, [0], [2, 3], 4, 0),
+    ('s2', 1, 0, 0, [0, 1], 0, 0),
+    ('s2', 1, 0, 1, [0, 1], 1, 0),
     ('sty', 'SP', 0, [0, 1, 2, 3], [0, 1]),
-    ('cast', 'S', 0, 0, 8),
-    ('stt', 0, [0], [2, 3], 0, 256),
-    ('stt', 0, [1], [2, 3], 1, 256),
+    ('s2', 1, 0, 2, [0, 1], 2, 0),
+    ('stt', 0, [1], [2, 3], 5, 0),
+    ('s2', 1, 0, 3, [0, 1], 3, 0),
+    ('cast', 'S', 0, 0, 8, [0, 1]),
+    ('s2', 1, 1, 0, [0, 1], 0, 0),
     ('qa', 3, 1),
-    ('stt', 0, [2], [2, 3], 2, 256),
-    ('stt', 0, [3], [2, 3], 3, 256),
+    ('s2', 1, 1, 1, [0, 1], 1, 0),
+    ('s2', 1, 1, 2, [0, 1], 2, 0),
+    ('s2', 1, 1, 3, [0, 1], 3, 0),
+    ('s2', 1, 2, 0, [0, 1], 0, 0),
+    ('s2', 1, 2, 1, [0, 1], 1, 0),
+    ('stt', 0, [2], [2, 3], 6, 0),
+    ('s2', 1, 2, 2, [0, 1], 2, 0),
+    ('s2', 1, 2, 3, [0, 1], 3, 0),
+    ('stt', 0, [3], [2, 3], 7, 0),
+    ('s2', 1, 3, 0, [0, 1], 0, 0),
+    ('s2', 1, 3, 1, [0, 1], 1, 0),
+    ('s2', 1, 3, 2, [0, 1], 2, 0),
+    ('stt', 1, [0], [0, 1], 0, 0),
+    ('s2', 1, 3, 3, [0, 1], 3, 0),
     ('sty', 'SP', 0, [0, 1, 2, 3], [2, 3]),
-    ('cast', 'S', 0, 8, 16),
+    ('cast', 'S', 0, 8, 16, [2, 3]),
+    ('s2', 1, 0, 0, [2], 4, 0),
+    ('s2', 1, 1, 0, [2], 4, 0),
+    ('s2', 1, 2, 0, [2], 4, 0),
+    ('stt', 1, [1], [0, 1], 1, 0),
+    ('s2', 1, 3, 0, [2], 4, 0),
+    ('s2', 1, 0, 1, [2], 5, 0),
+    ('s2', 1, 1, 1, [2], 5, 0),
+    ('stt', 1, [2], [0, 1], 2, 0),
+    ('s2', 1, 2, 1, [2], 5, 0),
+    ('s2', 1, 3, 1, [2], 5, 0),
+    ('s2', 1, 0, 2, [2], 6, 0),
+    ('s2', 1, 1, 2, [2], 6, 0),
+    ('stt', 1, [3], [0, 1], 3, 0),
+    ('s2', 1, 2, 2, [2], 6, 0),
+    ('s2', 1, 3, 2, [2], 6, 0),
+    ('s2', 1, 0, 3, [2], 7, 0),
+    ('s2', 1, 1, 3, [2], 7, 0),
     ('qy', 0, [0, 1]),
-    ('s2', 1, 3, 0, [0, 1], 4, 0),
-    ('s2', 1, 3, 1, [0, 1], 5, 0),
-    ('s2', 1, 3, 2, [0, 1], 6, 0),
-    ('s2', 1, 3, 3, [0, 1], 7, 0),
-    ('stt', 1, [0], [0, 1], 4, 0),
-    ('stt', 1, [1], [0, 1], 5, 0),
-    ('stt', 1, [2], [0, 1], 6, 0),
-    ('stt', 1, [3], [0, 1], 7, 0),
+    ('s2', 1, 2, 3, [2], 7, 0),
+    ('s2', 1, 3, 3, [2], 7, 0),
+    ('s2', 1, 0, 0, [3], 0, 0),
     ('sty', 'SP', 1, [0, 1, 2, 3], [0, 1]),
+    ('s2', 1, 1, 0, [3], 0, 0),
+    ('cast', 'S', 1, 0, 8, [0, 1]),
+    ('stt', 1, [0], [2], 4, 0),
+    ('s2', 1, 2, 0, [3], 0, 0),
+    ('s2', 1, 3, 0, [3], 0, 0),
+    ('stt', 1, [1], [2], 5, 0),
+    ('s2', 1, 0, 1, [3], 1, 0),
+    ('s2', 1, 1, 1, [3], 1, 0),
+    ('s2', 1, 2, 1, [3], 1, 0),
+    ('stt', 1, [2], [2], 6, 0),
+    ('s2', 1, 3, 1, [3], 1, 0),
+    ('s2', 1, 0, 2, [3], 2, 0),
+    ('stt', 1, [3], [2], 7, 0),
+    ('s2', 1, 1, 2, [3], 2, 0),
+    ('s2', 1, 2, 2, [3], 2, 0),
     ('qy', 0, [2, 3]),
-    ('stq', 'SP', 0, [0, 1, 2, 3]),
-    ('cast', 'S', 1, 0, 8),
-    ('s2', 1, 0, 0, [2], 0, 0),
-    ('s2', 1, 1, 0, [2], 0, 0),
-    ('s2', 1, 2, 0, [2], 0, 0),
-    ('s2', 1, 3, 0, [2], 0, 0),
-    ('s2', 1, 0, 1, [2], 1, 0),
-    ('s2', 1, 1, 1, [2], 1, 0),
-    ('s2', 1, 2, 1, [2], 1, 0),
-    ('s2', 1, 3, 1, [2], 1, 0),
-    ('s2', 1, 0, 2, [2], 2, 0),
-    ('s2', 1, 1, 2, [2], 2, 0),
-    ('s2', 1, 2, 2, [2], 2, 0),
-    ('s2', 1, 3, 2, [2], 2, 0),
-    ('s2', 1, 0, 3, [2], 3, 0),
-    ('s2', 1, 1, 3, [2], 3, 0),
-    ('s2', 1, 2, 3, [2], 3, 0),
-    ('s2', 1, 3, 3, [2], 3, 0),
-    ('stt', 1, [0], [2], 0, 0),
-    ('stt', 1, [1], [2], 1, 0),
-    ('stt', 1, [2], [2], 2, 0),
-    ('stt', 1, [3], [2], 3, 0),
+    ('s2', 1, 3, 2, [3], 2, 0),
+    ('s2', 1, 0, 3, [3], 3, 0),
+    ('s2', 1, 1, 3, [3], 3, 0),
     ('sty', 'SP', 1, [0, 1, 2, 3], [2]),
-    ('cast', 'S', 1, 8, 12),
-    ('s2', 1, 0, 0, [3], 4, 0),
-    ('s2', 1, 1, 0, [3], 4, 0),
-    ('s2', 1, 2, 0, [3], 4, 0),
-    ('s2', 1, 3, 0, [3], 4, 0),
-    ('s2', 1, 0, 1, [3], 5, 0),
-    ('s2', 1, 1, 1, [3], 5, 0),
-    ('s2', 1, 2, 1, [3], 5, 0),
-    ('s2', 1, 3, 1, [3], 5, 0),
-    ('s2', 1, 0, 2, [3], 6, 0),
-    ('s2', 1, 1, 2, [3], 6, 0),
-    ('s2', 1, 2, 2, [3], 6, 0),
-    ('s2', 1, 3, 2, [3], 6, 0),
-    ('s2', 1, 0, 3, [3], 7, 0),
-    ('s2', 1, 1, 3, [3], 7, 0),
-    ('s2', 1, 2, 3, [3], 7, 0),
-    ('s2', 1, 3, 3, [3], 7, 0),
-    ('stt', 1, [0], [3], 4, 0),
-    ('stt', 1, [1], [3], 5, 0),
-    ('stt', 1, [2], [3], 6, 0),
-    ('stt', 1, [3], [3], 7, 0),
-    ('sty', 'SP', 1, [0, 1, 2, 3], [3]),
+    ('s2', 1, 2, 3, [3], 3, 0),
+    ('stt', 1, [0], [3], 0, 0),
+    ('s2', 1, 3, 3, [3], 3, 0),
+    ('stt', 1, [1], [3], 1, 0),
+    ('stq', 'SP', 0, [0, 1, 2, 3]),
+    ('stt', 1, [2], [3], 2, 0),
+    ('cast', 'S', 1, 8, 12, [2]),
+    ('stt', 1, [3], [3], 3, 0),
     ('qy', 1, [0, 1]),
+    ('sty', 'SP', 1, [0, 1, 2, 3], [3]),
+    ('cast', 'V', 1, 12, 16, [3]),
     ('stq', 'SP', 1, [0, 1]),
-    ('cast', 'V', 1, 12, 16),
     ('qy', 1, [2]),
     ('qy', 1, [3]),
     ('stq', 'SP', 1, [2, 3]),
@@ -236,21 +254,21 @@ def tile_newton_schulz_factor_block_h2_kernel(tc, x_words, x_scales, a4_words, a
     with ExitStack() as ctx:
         sb = ctx.enter_context(tc.tile_pool(name="sb", bufs=1))
         ps = ctx.enter_context(tc.psum_pool(name="ps", bufs=1))
-        x_codes = sb.tile([128, 2, 512], U32, align_bytes=256)
+        x_codes = {i: sb.tile([128, 2, 256], U32, align_bytes=256, name="x_codes%d" % i) for i in range(2)}
         x_sc = sb.tile([128, 2, 512], U8, align_bytes=256)
-        w_codes = sb.tile([128, 2, 4096], U8, align_bytes=256)
-        h_t = sb.tile([128, 4, 4, 512], BF16, align_bytes=256)
+        w_codes = {i: sb.tile([128, 2, 1024], U8, align_bytes=256, name="w_codes%d" % i) for i in range(4)}
+        h_t = {(i, j): sb.tile([128, 512], BF16, align_bytes=256, name="h_t%d_%d" % (i, j)) for i in range(4) for j in range(4)}
         ident = sb.tile([128, 128], F32, align_bytes=256)
-        ws_raw = sb.tile([128, 2, 2048], U8, align_bytes=256)
-        a_raw = sb.tile([128, 4, 4, 1024], BF16, align_bytes=256)
-        a_il = sb.tile([128, 4, 2, 2048], BF16, align_bytes=256)
-        a_codes = sb.tile([128, 4, 2, 512], U32, align_bytes=256)
-        a_sc = sb.tile([128, 4, 2, 512], U8, align_bytes=256)
-        h_il = sb.tile([128, 4, 2048], BF16, align_bytes=256)
-        h_codes = sb.tile([128, 4, 512], U32, align_bytes=256)
-        h_sc = sb.tile([128, 4, 512], U8, align_bytes=256)
-        v_sb = sb.tile([128, 2, 4, 512], BF16, align_bytes=256)
-        y32 = sb.tile([128, 2, 4, 512], F32, align_bytes=256)
+        ws_raw = {i: sb.tile([128, 2, 1024], U8, align_bytes=256, name="ws_raw%d" % i) for i in range(2)}
+        a_raw = {(i, j): sb.tile([128, 4, 512], BF16, align_bytes=256, name="a_raw%d_%d" % (i, j)) for i in range(4) for j in range(2)}
+        a_il = {(i, j): sb.tile([128, 2048], BF16, align_bytes=256, name="a_il%d_%d" % (i, j)) for i in range(4) for j in range(2)}
+        a_codes = {(i, j): sb.tile([128, 512], U32, align_bytes=256, name="a_codes%d_%d" % (i, j)) for i in range(4) for j in range(2)}
+        a_sc = {(i, j): sb.tile([128, 512], U8, align_bytes=256, name="a_sc%d_%d" % (i, j)) for i in range(4) for j in range(2)}
+        h_il = {i: sb.tile([128, 2048], BF16, align_bytes=256, name="h_il%d" % i) for i in range(4)}
+        h_codes = {i: sb.tile([128, 512], U32, align_bytes=256, name="h_codes%d" % i) for i in range(4)}
+        h_sc = {i: sb.tile([128, 512], U8, align_bytes=256, name="h_sc%d" % i) for i in range(4)}
+        v_sb = {i: sb.tile([128, 4, 512], BF16, align_bytes=256, name="v_sb%d" % i) for i in range(2)}
+        y32 = {(i, j): sb.tile([128, 1024], F32, align_bytes=256, name="y32%d_%d" % (i, j)) for i in range(2) for j in range(4)}
         y_il = sb.tile([128, 2, 2048], BF16, align_bytes=256)
         y_codes = sb.tile([128, 2, 512], U32, align_bytes=256)
         y_sc = sb.tile([128, 2, 512], U8, align_bytes=256)
@@ -265,6 +283,9 @@ def tile_newton_schulz_factor_block_h2_kernel(tc, x_words, x_scales, a4_words, a
             banks[b] = ps.tile([128, 512], F32, name="bank%d" % b, tag="bank%d" % b)
             return banks[b]
 
+        def y_unit(g, c0, c1):
+            return y32[g, c0 // 128][:, : 4 * (c1 - c0)].rearrange("p (t m) -> p t m", t=4)
+
         def copy(e, out, in_):
             if e == "V":
                 nc.vector.tensor_copy(out=out, in_=in_)
@@ -275,8 +296,8 @@ def tile_newton_schulz_factor_block_h2_kernel(tc, x_words, x_scales, a4_words, a
         for st in PROGRAM:
             k = st[0]
             if k == "ms":
-                t = x_sc if st[2] == "msx" else ws_raw
-                eng[st[1]].memset(t[:].rearrange("p g n -> p (g n)").bitcast(I32), 0)
+                t = x_sc[:] if st[2] == "msx" else ws_raw[int(st[2][3])][:]
+                eng[st[1]].memset(t.rearrange("p g n -> p (g n)").bitcast(I32), 0)
             elif k == "act0":
                 nc.gpsimd.memset(prime[:], 0.0)
                 nc.scalar.activation(out=prime2[:], in_=prime[:], func=ACT.Copy, scale=0.5)
@@ -291,7 +312,7 @@ def tile_newton_schulz_factor_block_h2_kernel(tc, x_words, x_scales, a4_words, a
                     nc.tensor.matmul_mx(out=bank[:, :n], lhsT=wu_codes[:, :128].bitcast(FP8X4), lhsT_scale=wu_sc[:, :128],
                                         rhs=wu_codes[:, :n].bitcast(FP8X4), rhs_scale=wu_sc[:, :n], start=True, stop=True)
             elif k == "ldx":
-                eng[st[1]].dma_start(out=x_codes[:].bitcast(I32), in_=x_words.rearrange("g p n t -> p g (n t)").bitcast(I32))
+                eng[st[1]].dma_start(out=x_codes[st[2]][:].bitcast(I32), in_=x_words.rearrange("g p n t -> p g (n t)").bitcast(I32)[:, :, 256 * st[2] : 256 * (st[2] + 1)])
             elif k == "ldxs":
                 r = st[2]
                 eng[st[1]].dma_start(out=x_sc[r:128:32, :, :].bitcast(I32),
@@ -299,34 +320,34 @@ def tile_newton_schulz_factor_block_h2_kernel(tc, x_words, x_scales, a4_words, a
             elif k == "ldws":
                 r = st[2]
                 cols = slice(512 * st[3][0], 512 * (st[3][-1] + 1))
-                eng[st[1]].dma_start(out=ws_raw[r:128:32, :, cols].bitcast(I32),
+                eng[st[1]].dma_start(out=ws_raw[st[3][0] // 2][r:128:32, :, :].bitcast(I32),
                                      in_=a4_scales.rearrange("g (q r) n -> r q g n", r=4)[r][:, :, cols].bitcast(I32))
             elif k == "ldw":
                 for G in st[2]:
-                    eng[st[1]].dma_start(out=w_codes[:, :, 1024 * G : 1024 * (G + 1)].bitcast(I32),
+                    eng[st[1]].dma_start(out=w_codes[G][:].bitcast(I32),
                                          in_=a4_words[:, :, 1024 * G : 1024 * (G + 1)].rearrange("g p n -> p g n").bitcast(I32))
             elif k == "lda":
                 G, gs = st[2], st[3]
                 cols = slice(512 * gs[0], 512 * (gs[-1] + 1))
                 rows = a[512 * G : 512 * (G + 1), :].rearrange("(p j) q -> p j q", j=4)
-                eng[st[1]].dma_start(out=a_raw[:, G, :, cols], in_=rows[:, :, cols])
+                eng[st[1]].dma_start(out=a_raw[G, gs[0]][:], in_=rows[:, :, cols])
             elif k == "ident":
                 make_identity(nc, ident[:])
             elif k == "ldv":
                 for g in st[2]:
-                    eng[st[1]].dma_start(out=v_sb[:, g, :, :], in_=v[512 * g : 512 * (g + 1), :].rearrange("(p t) m -> p t m", t=4))
+                    eng[st[1]].dma_start(out=v_sb[g][:, :, :], in_=v[512 * g : 512 * (g + 1), :].rearrange("(p t) m -> p t m", t=4))
             elif k == "s1":
                 G, c = st[1], st[2]
                 bank = new_bank(st[3])
                 for gk in range(2):
                     nc.tensor.matmul_mx(out=bank[:],
-                                        lhsT=x_codes[:, gk, 128 * c : 128 * (c + 1)].bitcast(FP8X4), lhsT_scale=x_sc[:, gk, 128 * c : 128 * (c + 1)],
-                                        rhs=w_codes[:, gk, 1024 * G : 1024 * (G + 1)].bitcast(FP4X4),
-                                        rhs_scale=ws_raw[:, gk, 512 * G : 512 * (G + 1)], start=(gk == 0), stop=(gk == 1))
+                                        lhsT=x_codes[c // 2][:, gk, 128 * (c % 2) : 128 * (c % 2 + 1)].bitcast(FP8X4), lhsT_scale=x_sc[:, gk, 128 * c : 128 * (c + 1)],
+                                        rhs=w_codes[G][:, gk, :].bitcast(FP4X4),
+                                        rhs_scale=ws_raw[G // 2][:, gk, 512 * (G % 2) : 512 * (G % 2 + 1)], start=(gk == 0), stop=(gk == 1))
             elif k == "ev":
                 e, G, c = st[1], st[2], st[3]
                 src = banks[st[4]][:].rearrange("m (p u e) -> m u p e", u=2, e=2)
-                dst = h_t[:, G, c, :].rearrange("m (u p e) -> m u p e", u=2, e=2)
+                dst = h_t[G, c][:].rearrange("m (u p e) -> m u p e", u=2, e=2)
                 if e == "S":
                     nc.scalar.activation(out=dst, in_=src, func=ACT.Copy, scale=0.5)
                 else:
@@ -335,26 +356,26 @@ def tile_newton_schulz_factor_block_h2_kernel(tc, x_words, x_scales, a4_words, a
                 G, h = st[1], st[2]
                 bank = new_bank(st[3])
                 for cc in range(2):
-                    words = h_t[:, G, 2 * h + cc, :].bitcast(F32)
+                    words = h_t[G, 2 * h + cc][:].bitcast(F32)
                     for u in range(2):
                         i = 2 * cc + u
                         nc.tensor.transpose(bank[:, 128 * i : 128 * (i + 1)], words[:, 128 * u : 128 * (u + 1)], ident[:])
             elif k == "cp":
                 e, G, h = st[1], st[2], st[3]
                 src = banks[st[4]][:].rearrange("p (c u m) -> p c m u", c=2, u=2)
-                dst = h_il[:, G, 1024 * h : 1024 * (h + 1)].bitcast(F32).rearrange("p (c m u) -> p c m u", c=2, u=2)
+                dst = h_il[G][:, 1024 * h : 1024 * (h + 1)].bitcast(F32).rearrange("p (c m u) -> p c m u", c=2, u=2)
                 copy(e, dst, src)
             elif k == "il":
-                e, G, g, m0, m1 = st[1], st[2], st[3], 16 * st[4], 16 * st[5]
-                src = a_raw[:, G, :, 512 * g + 4 * m0 : 512 * g + 4 * m1].rearrange("p j (m e t) -> p m t e j", t=4, e=2)
-                dst = a_il[:, G, g, :].rearrange("p (t m e j) -> p m t e j", t=4, e=2, j=4)[:, m0 // 2 : m1 // 2, :, :, :]
+                e, G, g, t0, t1 = st[1], st[2], st[3], st[4] // 2, st[5] // 2
+                src = a_raw[G, g][:].rearrange("p j (m e t) -> p m t e j", t=4, e=2)[:, :, t0:t1, :, :]
+                dst = a_il[G, g][:, 512 * t0 : 512 * t1].rearrange("p (t m e j) -> p m t e j", t=t1 - t0, e=2, j=4)
                 copy(e, dst, src)
             elif k == "qa":
                 G, g = st[1], st[2]
-                nc.vector.quantize_mx(out=a_codes[:, G, g, :].bitcast(FP8X4), scales=a_sc[:, G, g, :], in_=a_il[:, G, g, :])
+                nc.vector.quantize_mx(out=a_codes[G, g][:, :].bitcast(FP8X4), scales=a_sc[G, g][:, :], in_=a_il[G, g][:, :])
             elif k == "qh":
                 G, c0, c1 = st[1], 128 * st[2][0], 128 * (st[2][-1] + 1)
-                nc.vector.quantize_mx(out=h_codes[:, G, c0:c1].bitcast(FP8X4), scales=h_sc[:, G, c0:c1], in_=h_il[:, G, 4 * c0 : 4 * c1])
+                nc.vector.quantize_mx(out=h_codes[G][:, c0:c1].bitcast(FP8X4), scales=h_sc[G][:, c0:c1], in_=h_il[G][:, 4 * c0 : 4 * c1])
             elif k == "s2":
                 g, G, t, cs, b = st[1:6]
                 c0, c1 = 128 * cs[0], 128 * (cs[-1] + 1)
@@ -363,9 +384,9 @@ def tile_newton_schulz_factor_block_h2_kernel(tc, x_words, x_scales, a4_words, a
                 if G == 0 and slot == 0:
                     new_bank(b)
                 nc.tensor.matmul_mx(out=banks[b][:, n * slot : n * (slot + 1)],
-                                    lhsT=a_codes[:, G, g, 128 * t : 128 * (t + 1)].bitcast(FP8X4),
-                                    lhsT_scale=a_sc[:, G, g, 128 * t : 128 * (t + 1)],
-                                    rhs=h_codes[:, G, c0:c1].bitcast(FP8X4), rhs_scale=h_sc[:, G, c0:c1],
+                                    lhsT=a_codes[G, g][:, 128 * t : 128 * (t + 1)].bitcast(FP8X4),
+                                    lhsT_scale=a_sc[G, g][:, 128 * t : 128 * (t + 1)],
+                                    rhs=h_codes[G][:, c0:c1].bitcast(FP8X4), rhs_scale=h_sc[G][:, c0:c1],
                                     start=(G == 0), stop=(G == 3))
             elif k == "stt":
                 g, ts, cs, b, off = st[1:6]
@@ -373,12 +394,13 @@ def tile_newton_schulz_factor_block_h2_kernel(tc, x_words, x_scales, a4_words, a
                 n = c1 - c0
                 t0, t1 = ts[0], ts[-1] + 1
                 src = banks[b][:, off : off + n * len(ts)].rearrange("p (t m) -> p t m", t=len(ts))
-                nc.vector.scalar_tensor_tensor(out=y32[:, g, t0:t1, c0:c1], in0=v_sb[:, g, t0:t1, c0:c1], scalar=1.5, in1=src,
+                nc.vector.scalar_tensor_tensor(out=y_unit(g, c0, c1)[:, t0:t1, :], in0=v_sb[g][:, t0:t1, c0:c1], scalar=1.5, in1=src,
                                                op0=ALU.mult, op1=ALU.subtract)
             elif k == "cast":
                 e, g, m0, m1 = st[1], st[2], 32 * st[3], 32 * st[4]
-                src = y32[:, g, :, m0:m1].rearrange("p t (c i) -> p c t i", i=4)
-                dst = y_il[:, g, 4 * m0 : 4 * m1].rearrange("p (c i t) -> p c t i", i=4, t=4)
+                c0, c1 = 128 * st[5][0], 128 * (st[5][-1] + 1)
+                src = y_unit(g, c0, c1)[:, :, m0 - c0 : m1 - c0].rearrange("p t m -> p m t")
+                dst = y_il[:, g, 4 * m0 : 4 * m1].rearrange("p (m t) -> p m t", t=4)
                 copy(e, dst, src)
             elif k == "qy":
                 g, c0, c1 = st[1], 128 * st[2][0], 128 * (st[2][-1] + 1)
@@ -388,7 +410,7 @@ def tile_newton_schulz_factor_block_h2_kernel(tc, x_words, x_scales, a4_words, a
                 c0, c1 = 128 * cs[0], 128 * (cs[-1] + 1)
                 t0, t1 = ts[0], ts[-1] + 1
                 dst = out_0[512 * g : 512 * (g + 1), :].rearrange("(p t) m -> p t m", t=4)
-                eng[st[1]].dma_start(out=dst[:, t0:t1, c0:c1], in_=y32[:, g, t0:t1, c0:c1])
+                eng[st[1]].dma_start(out=dst[:, t0:t1, c0:c1], in_=y_unit(g, c0, c1)[:, t0:t1, :])
             elif k == "stq":
                 g, c0, c1 = st[2], 128 * st[3][0], 128 * (st[3][-1] + 1)
                 dst = out_1[g].rearrange("p m t -> p (m t)").bitcast(I32)

from contextlib import ExitStack

import concourse.mybir as mybir
from concourse.masks import make_identity

F32 = mybir.dt.float32
BF16 = mybir.dt.bfloat16
I32 = mybir.dt.int32
U32 = mybir.dt.uint32
U8 = mybir.dt.uint8
FP8X4 = mybir.dt.float8_e4m3fn_x4
FP4X4 = mybir.dt.float4_e2m1fn_x4
ALU = mybir.AluOpType
ACT = mybir.ActivationFunctionType

FLOPS = 2 * 2 * 2048 * 1024 * 512

PROGRAM = [
    ('ms', 'G', 'msx', 256),
    ('ident',),
    ('ms', 'V', 'msw0', 512),
    ('ldxs', 'SP', 0),
    ('act0',),
    ('ldxs', 'SP', 1),
    ('ldxs', 'SP', 2),
    ('ldxs', 'SP', 3),
    ('wuq', 128),
    ('lda', 'SP', 0, (0,)),
    ('ldx', 'SP', 0),
    ('ldw', 'SP', (0,)),
    ('ldws', 'SP', 0, (0, 1)),
    ('ms', 'V', 'msw1', 512),
    ('wu', 128, 25, 7),
    ('ldws', 'SP', 1, (0, 1)),
    ('ldws', 'SP', 2, (0, 1)),
    ('ldws', 'SP', 3, (0, 1)),
    ('ldx', 'SP', 1),
    ('lda', 'SP', 0, (1,)),
    ('il', 'V', 0, 0, 0, 6),
    ('il', 'S', 0, 0, 6, 8),
    ('ldw', 'SP', (1,)),
    ('lda', 'SP', 1, (0,)),
    ('ldws', 'SP', 0, (2, 3)),
    ('qa', 0, 0),
    ('ldws', 'SP', 1, (2, 3)),
    ('ldws', 'SP', 2, (2, 3)),
    ('ldws', 'SP', 3, (2, 3)),
    ('s1', 0, 0, 0),
    ('ldw', 'SP', (2,)),
    ('s1', 0, 1, 1),
    ('ev', 'S', 0, 0, 0),
    ('s1', 0, 2, 2),
    ('ev', 'S', 0, 1, 1),
    ('lda', 'SP', 2, (0,)),
    ('il', 'V', 0, 1, 0, 8),
    ('s1', 0, 3, 3),
    ('ev', 'S', 0, 2, 2),
    ('lda', 'SP', 1, (1,)),
    ('s1', 1, 0, 0),
    ('ev', 'S', 0, 3, 3),
    ('s1', 1, 1, 1),
    ('ev', 'S', 1, 0, 0),
    ('ldw', 'SP', (3,)),
    ('il', 'V', 1, 0, 0, 8),
    ('s1', 1, 2, 2),
    ('lda', 'SP', 3, (0,)),
    ('lda', 'SP', 2, (1,)),
    ('ev', 'S', 1, 1, 1),
    ('ldv', 'SP', (0,)),
    ('s1', 1, 3, 3),
    ('lda', 'SP', 3, (1,)),
    ('ev', 'S', 1, 2, 2),
    ('tr', 0, 0, 4, 1),
    ('ldv', 'SP', (1,)),
    ('qa', 0, 1),
    ('ev', 'S', 1, 3, 3),
    ('tr', 0, 1, 5, 1),
    ('qa', 1, 0),
    ('s1', 2, 0, 0),
    ('cp', 'S', 0, 0, 4),
    ('il', 'V', 2, 0, 0, 8),
    ('s1', 2, 1, 1),
    ('cp', 'S', 0, 1, 5),
    ('s1', 2, 2, 2),
    ('ev', 'S', 2, 0, 0),
    ('s1', 2, 3, 3),
    ('ev', 'S', 2, 1, 1),
    ('qh', 0, [0, 1, 2, 3]),
    ('tr', 1, 0, 6, 1),
    ('ev', 'S', 2, 2, 2),
    ('qa', 2, 0),
    ('tr', 1, 1, 7, 1),
    ('ev', 'S', 2, 3, 3),
    ('il', 'V', 1, 1, 0, 8),
    ('s1', 3, 0, 0),
    ('cp', 'S', 1, 0, 6),
    ('s1', 3, 1, 1),
    ('cp', 'S', 1, 1, 7),
    ('s1', 3, 2, 2),
    ('il', 'V', 3, 0, 0, 8),
    ('ev', 'S', 3, 0, 0),
    ('s1', 3, 3, 3),
    ('ev', 'S', 3, 1, 1),
    ('tr', 2, 0, 4, 1),
    ('ev', 'S', 3, 2, 2),
    ('qh', 1, [0, 1, 2, 3]),
    ('tr', 2, 1, 5, 1),
    ('s2', 0, 0, 0, [0, 1], 0, 0),
    ('ev', 'S', 3, 3, 3),
    ('qa', 3, 0),
    ('s2', 0, 0, 1, [0, 1], 1, 0),
    ('s2', 0, 0, 2, [0, 1], 2, 0),
    ('s2', 0, 1, 0, [0, 1], 0, 0),
    ('s2', 0, 1, 1, [0, 1], 1, 0),
    ('cp', 'S', 2, 0, 4),
    ('il', 'V', 2, 1, 0, 6),
    ('s2', 0, 1, 2, [0, 1], 2, 0),
    ('tr', 3, 0, 6, 1),
    ('cp', 'S', 2, 1, 5),
    ('tr', 3, 1, 7, 1),
    ('cp', 'S', 3, 0, 6),
    ('s2', 0, 0, 3, [0, 1], 3, 0),
    ('s2', 0, 1, 3, [0, 1], 3, 0),
    ('qh', 2, [0, 1, 2, 3]),
    ('s2', 0, 0, 0, [2, 3], 4, 0),
    ('s2', 0, 0, 1, [2, 3], 5, 0),
    ('cp', 'S', 3, 1, 7),
    ('s2', 0, 1, 0, [2, 3], 4, 0),
    ('s2', 0, 1, 1, [2, 3], 5, 0),
    ('qa', 1, 1),
    ('s2', 0, 2, 0, [0, 1], 0, 0),
    ('il', 'S', 2, 1, 6, 8),
    ('s2', 0, 2, 1, [0, 1], 1, 0),
    ('s2', 0, 2, 2, [0, 1], 2, 0),
    ('qh', 3, [0, 1]),
    ('s2', 0, 2, 3, [0, 1], 3, 0),
    ('s2', 0, 0, 2, [2, 3], 6, 0),
    ('qh', 3, [2, 3]),
    ('s2', 0, 0, 3, [2, 3], 7, 0),
    ('il', 'S', 3, 1, 0, 8),
    ('s2', 0, 1, 2, [2, 3], 6, 0),
    ('qa', 2, 1),
    ('s2', 0, 1, 3, [2, 3], 7, 0),
    ('s2', 0, 3, 0, [0, 1], 0, 0),
    ('s2', 0, 3, 1, [0, 1], 1, 0),
    ('s2', 0, 3, 2, [0, 1], 2, 0),
    ('s2', 0, 3, 3, [0, 1], 3, 0),
    ('stt', 0, [0], [0, 1], 0, 0),
    ('s2', 0, 2, 0, [2, 3], 4, 0),
    ('s2', 0, 2, 1, [2, 3], 5, 0),
    ('stt', 0, [1], [0, 1], 1, 0),
    ('s2', 0, 2, 2, [2, 3], 6, 0),
    ('s2', 0, 2, 3, [2, 3], 7, 0),
    ('stt', 0, [2], [0, 1], 2, 0),
    ('s2', 0, 3, 0, [2, 3], 4, 0),
    ('s2', 0, 3, 1, [2, 3], 5, 0),
    ('stt', 0, [3], [0, 1], 3, 0),
    ('s2', 0, 3, 2, [2, 3], 6, 0),
    ('s2', 0, 3, 3, [2, 3], 7, 0),
    ('stt', 0, [0], [2, 3], 4, 0),
    ('s2', 1, 0, 0, [0, 1], 0, 0),
    ('s2', 1, 0, 1, [0, 1], 1, 0),
    ('sty', 'SP', 0, [0, 1, 2, 3], [0, 1]),
    ('s2', 1, 0, 2, [0, 1], 2, 0),
    ('stt', 0, [1], [2, 3], 5, 0),
    ('s2', 1, 0, 3, [0, 1], 3, 0),
    ('cast', 'S', 0, 0, 8, [0, 1]),
    ('s2', 1, 1, 0, [0, 1], 0, 0),
    ('qa', 3, 1),
    ('s2', 1, 1, 1, [0, 1], 1, 0),
    ('s2', 1, 1, 2, [0, 1], 2, 0),
    ('s2', 1, 1, 3, [0, 1], 3, 0),
    ('s2', 1, 2, 0, [0, 1], 0, 0),
    ('s2', 1, 2, 1, [0, 1], 1, 0),
    ('stt', 0, [2], [2, 3], 6, 0),
    ('s2', 1, 2, 2, [0, 1], 2, 0),
    ('s2', 1, 2, 3, [0, 1], 3, 0),
    ('stt', 0, [3], [2, 3], 7, 0),
    ('s2', 1, 3, 0, [0, 1], 0, 0),
    ('s2', 1, 3, 1, [0, 1], 1, 0),
    ('s2', 1, 3, 2, [0, 1], 2, 0),
    ('stt', 1, [0], [0, 1], 0, 0),
    ('s2', 1, 3, 3, [0, 1], 3, 0),
    ('sty', 'SP', 0, [0, 1, 2, 3], [2, 3]),
    ('cast', 'S', 0, 8, 16, [2, 3]),
    ('s2', 1, 0, 0, [2], 4, 0),
    ('s2', 1, 1, 0, [2], 4, 0),
    ('s2', 1, 2, 0, [2], 4, 0),
    ('stt', 1, [1], [0, 1], 1, 0),
    ('s2', 1, 3, 0, [2], 4, 0),
    ('s2', 1, 0, 1, [2], 5, 0),
    ('s2', 1, 1, 1, [2], 5, 0),
    ('stt', 1, [2], [0, 1], 2, 0),
    ('s2', 1, 2, 1, [2], 5, 0),
    ('s2', 1, 3, 1, [2], 5, 0),
    ('s2', 1, 0, 2, [2], 6, 0),
    ('s2', 1, 1, 2, [2], 6, 0),
    ('stt', 1, [3], [0, 1], 3, 0),
    ('s2', 1, 2, 2, [2], 6, 0),
    ('s2', 1, 3, 2, [2], 6, 0),
    ('s2', 1, 0, 3, [2], 7, 0),
    ('s2', 1, 1, 3, [2], 7, 0),
    ('qy', 0, [0, 1]),
    ('s2', 1, 2, 3, [2], 7, 0),
    ('s2', 1, 3, 3, [2], 7, 0),
    ('s2', 1, 0, 0, [3], 0, 0),
    ('sty', 'SP', 1, [0, 1, 2, 3], [0, 1]),
    ('s2', 1, 1, 0, [3], 0, 0),
    ('cast', 'S', 1, 0, 8, [0, 1]),
    ('stt', 1, [0], [2], 4, 0),
    ('s2', 1, 2, 0, [3], 0, 0),
    ('s2', 1, 3, 0, [3], 0, 0),
    ('stt', 1, [1], [2], 5, 0),
    ('s2', 1, 0, 1, [3], 1, 0),
    ('s2', 1, 1, 1, [3], 1, 0),
    ('s2', 1, 2, 1, [3], 1, 0),
    ('stt', 1, [2], [2], 6, 0),
    ('s2', 1, 3, 1, [3], 1, 0),
    ('s2', 1, 0, 2, [3], 2, 0),
    ('stt', 1, [3], [2], 7, 0),
    ('s2', 1, 1, 2, [3], 2, 0),
    ('s2', 1, 2, 2, [3], 2, 0),
    ('qy', 0, [2, 3]),
    ('s2', 1, 3, 2, [3], 2, 0),
    ('s2', 1, 0, 3, [3], 3, 0),
    ('s2', 1, 1, 3, [3], 3, 0),
    ('sty', 'SP', 1, [0, 1, 2, 3], [2]),
    ('s2', 1, 2, 3, [3], 3, 0),
    ('stt', 1, [0], [3], 0, 0),
    ('s2', 1, 3, 3, [3], 3, 0),
    ('stt', 1, [1], [3], 1, 0),
    ('stq', 'SP', 0, [0, 1, 2, 3]),
    ('stt', 1, [2], [3], 2, 0),
    ('cast', 'S', 1, 8, 12, [2]),
    ('stt', 1, [3], [3], 3, 0),
    ('qy', 1, [0, 1]),
    ('sty', 'SP', 1, [0, 1, 2, 3], [3]),
    ('cast', 'V', 1, 12, 16, [3]),
    ('stq', 'SP', 1, [0, 1]),
    ('qy', 1, [2]),
    ('qy', 1, [3]),
    ('stq', 'SP', 1, [2, 3]),
    ('sts', 'S', (0, 1), 0),
    ('sts', 'SP', (0, 1), 1),
    ('sts', 'S', (0, 1), 2),
    ('sts', 'SP', (0, 1), 3),

]


def tile_newton_schulz_factor_block_h2_kernel(tc, x_words, x_scales, a4_words, a4_scales, a, v, out_0, out_1, out_2):
    nc = tc.nc
    eng = {"V": nc.vector, "S": nc.scalar, "SP": nc.sync, "G": nc.gpsimd}
    with ExitStack() as ctx:
        sb = ctx.enter_context(tc.tile_pool(name="sb", bufs=1))
        ps = ctx.enter_context(tc.psum_pool(name="ps", bufs=1))
        x_codes = {i: sb.tile([128, 2, 256], U32, align_bytes=256, name="x_codes%d" % i) for i in range(2)}
        x_sc = sb.tile([128, 2, 512], U8, align_bytes=256)
        w_codes = {i: sb.tile([128, 2, 1024], U8, align_bytes=256, name="w_codes%d" % i) for i in range(4)}
        h_t = {(i, j): sb.tile([128, 512], BF16, align_bytes=256, name="h_t%d_%d" % (i, j)) for i in range(4) for j in range(4)}
        ident = sb.tile([128, 128], F32, align_bytes=256)
        ws_raw = {i: sb.tile([128, 2, 1024], U8, align_bytes=256, name="ws_raw%d" % i) for i in range(2)}
        a_raw = {(i, j): sb.tile([128, 4, 512], BF16, align_bytes=256, name="a_raw%d_%d" % (i, j)) for i in range(4) for j in range(2)}
        a_il = {(i, j): sb.tile([128, 2048], BF16, align_bytes=256, name="a_il%d_%d" % (i, j)) for i in range(4) for j in range(2)}
        a_codes = {(i, j): sb.tile([128, 512], U32, align_bytes=256, name="a_codes%d_%d" % (i, j)) for i in range(4) for j in range(2)}
        a_sc = {(i, j): sb.tile([128, 512], U8, align_bytes=256, name="a_sc%d_%d" % (i, j)) for i in range(4) for j in range(2)}
        h_il = {i: sb.tile([128, 2048], BF16, align_bytes=256, name="h_il%d" % i) for i in range(4)}
        h_codes = {i: sb.tile([128, 512], U32, align_bytes=256, name="h_codes%d" % i) for i in range(4)}
        h_sc = {i: sb.tile([128, 512], U8, align_bytes=256, name="h_sc%d" % i) for i in range(4)}
        v_sb = {i: sb.tile([128, 4, 512], BF16, align_bytes=256, name="v_sb%d" % i) for i in range(2)}
        y32 = {(i, j): sb.tile([128, 1024], F32, align_bytes=256, name="y32%d_%d" % (i, j)) for i in range(2) for j in range(4)}
        y_il = sb.tile([128, 2, 2048], BF16, align_bytes=256)
        y_codes = sb.tile([128, 2, 512], U32, align_bytes=256)
        y_sc = sb.tile([128, 2, 512], U8, align_bytes=256)
        prime = sb.tile([128, 8], F32, align_bytes=256)
        prime2 = sb.tile([128, 8], F32, align_bytes=256)
        wu_in = sb.tile([128, 2048], BF16, align_bytes=256)
        wu_codes = sb.tile([128, 512], U32, align_bytes=256)
        wu_sc = sb.tile([128, 512], U8, align_bytes=256)
        banks = {}

        def new_bank(b):
            banks[b] = ps.tile([128, 512], F32, name="bank%d" % b, tag="bank%d" % b)
            return banks[b]

        def y_unit(g, c0, c1):
            return y32[g, c0 // 128][:, : 4 * (c1 - c0)].rearrange("p (t m) -> p t m", t=4)

        def copy(e, out, in_):
            if e == "V":
                nc.vector.tensor_copy(out=out, in_=in_)
            else:
                nc.scalar.copy(out=out, in_=in_)

        ctx.enter_context(tc.manual_schedule())
        for st in PROGRAM:
            k = st[0]
            if k == "ms":
                t = x_sc[:] if st[2] == "msx" else ws_raw[int(st[2][3])][:]
                eng[st[1]].memset(t.rearrange("p g n -> p (g n)").bitcast(I32), 0)
            elif k == "act0":
                nc.gpsimd.memset(prime[:], 0.0)
                nc.scalar.activation(out=prime2[:], in_=prime[:], func=ACT.Copy, scale=0.5)
            elif k == "wuq":
                n = st[1]
                nc.vector.memset(wu_in[:, : 4 * n].bitcast(I32), 0)
                nc.vector.quantize_mx(out=wu_codes[:, :n].bitcast(FP8X4), scales=wu_sc[:, :n], in_=wu_in[:, : 4 * n])
            elif k == "wu":
                n = st[1]
                bank = new_bank(st[3])
                for i in range(st[2]):
                    nc.tensor.matmul_mx(out=bank[:, :n], lhsT=wu_codes[:, :128].bitcast(FP8X4), lhsT_scale=wu_sc[:, :128],
                                        rhs=wu_codes[:, :n].bitcast(FP8X4), rhs_scale=wu_sc[:, :n], start=True, stop=True)
            elif k == "ldx":
                eng[st[1]].dma_start(out=x_codes[st[2]][:].bitcast(I32), in_=x_words.rearrange("g p n t -> p g (n t)").bitcast(I32)[:, :, 256 * st[2] : 256 * (st[2] + 1)])
            elif k == "ldxs":
                r = st[2]
                eng[st[1]].dma_start(out=x_sc[r:128:32, :, :].bitcast(I32),
                                     in_=x_scales.rearrange("g (q r) n -> r q g n", r=4)[r].bitcast(I32))
            elif k == "ldws":
                r = st[2]
                cols = slice(512 * st[3][0], 512 * (st[3][-1] + 1))
                eng[st[1]].dma_start(out=ws_raw[st[3][0] // 2][r:128:32, :, :].bitcast(I32),
                                     in_=a4_scales.rearrange("g (q r) n -> r q g n", r=4)[r][:, :, cols].bitcast(I32))
            elif k == "ldw":
                for G in st[2]:
                    eng[st[1]].dma_start(out=w_codes[G][:].bitcast(I32),
                                         in_=a4_words[:, :, 1024 * G : 1024 * (G + 1)].rearrange("g p n -> p g n").bitcast(I32))
            elif k == "lda":
                G, gs = st[2], st[3]
                cols = slice(512 * gs[0], 512 * (gs[-1] + 1))
                rows = a[512 * G : 512 * (G + 1), :].rearrange("(p j) q -> p j q", j=4)
                eng[st[1]].dma_start(out=a_raw[G, gs[0]][:], in_=rows[:, :, cols])
            elif k == "ident":
                make_identity(nc, ident[:])
            elif k == "ldv":
                for g in st[2]:
                    eng[st[1]].dma_start(out=v_sb[g][:, :, :], in_=v[512 * g : 512 * (g + 1), :].rearrange("(p t) m -> p t m", t=4))
            elif k == "s1":
                G, c = st[1], st[2]
                bank = new_bank(st[3])
                for gk in range(2):
                    nc.tensor.matmul_mx(out=bank[:],
                                        lhsT=x_codes[c // 2][:, gk, 128 * (c % 2) : 128 * (c % 2 + 1)].bitcast(FP8X4), lhsT_scale=x_sc[:, gk, 128 * c : 128 * (c + 1)],
                                        rhs=w_codes[G][:, gk, :].bitcast(FP4X4),
                                        rhs_scale=ws_raw[G // 2][:, gk, 512 * (G % 2) : 512 * (G % 2 + 1)], start=(gk == 0), stop=(gk == 1))
            elif k == "ev":
                e, G, c = st[1], st[2], st[3]
                src = banks[st[4]][:].rearrange("m (p u e) -> m u p e", u=2, e=2)
                dst = h_t[G, c][:].rearrange("m (u p e) -> m u p e", u=2, e=2)
                if e == "S":
                    nc.scalar.activation(out=dst, in_=src, func=ACT.Copy, scale=0.5)
                else:
                    nc.vector.tensor_scalar_mul(out=dst, in0=src, scalar1=0.5)
            elif k == "tr":
                G, h = st[1], st[2]
                bank = new_bank(st[3])
                for cc in range(2):
                    words = h_t[G, 2 * h + cc][:].bitcast(F32)
                    for u in range(2):
                        i = 2 * cc + u
                        nc.tensor.transpose(bank[:, 128 * i : 128 * (i + 1)], words[:, 128 * u : 128 * (u + 1)], ident[:])
            elif k == "cp":
                e, G, h = st[1], st[2], st[3]
                src = banks[st[4]][:].rearrange("p (c u m) -> p c m u", c=2, u=2)
                dst = h_il[G][:, 1024 * h : 1024 * (h + 1)].bitcast(F32).rearrange("p (c m u) -> p c m u", c=2, u=2)
                copy(e, dst, src)
            elif k == "il":
                e, G, g, t0, t1 = st[1], st[2], st[3], st[4] // 2, st[5] // 2
                src = a_raw[G, g][:].rearrange("p j (m e t) -> p m t e j", t=4, e=2)[:, :, t0:t1, :, :]
                dst = a_il[G, g][:, 512 * t0 : 512 * t1].rearrange("p (t m e j) -> p m t e j", t=t1 - t0, e=2, j=4)
                copy(e, dst, src)
            elif k == "qa":
                G, g = st[1], st[2]
                nc.vector.quantize_mx(out=a_codes[G, g][:, :].bitcast(FP8X4), scales=a_sc[G, g][:, :], in_=a_il[G, g][:, :])
            elif k == "qh":
                G, c0, c1 = st[1], 128 * st[2][0], 128 * (st[2][-1] + 1)
                nc.vector.quantize_mx(out=h_codes[G][:, c0:c1].bitcast(FP8X4), scales=h_sc[G][:, c0:c1], in_=h_il[G][:, 4 * c0 : 4 * c1])
            elif k == "s2":
                g, G, t, cs, b = st[1:6]
                c0, c1 = 128 * cs[0], 128 * (cs[-1] + 1)
                n = c1 - c0
                slot = st[6]
                if G == 0 and slot == 0:
                    new_bank(b)
                nc.tensor.matmul_mx(out=banks[b][:, n * slot : n * (slot + 1)],
                                    lhsT=a_codes[G, g][:, 128 * t : 128 * (t + 1)].bitcast(FP8X4),
                                    lhsT_scale=a_sc[G, g][:, 128 * t : 128 * (t + 1)],
                                    rhs=h_codes[G][:, c0:c1].bitcast(FP8X4), rhs_scale=h_sc[G][:, c0:c1],
                                    start=(G == 0), stop=(G == 3))
            elif k == "stt":
                g, ts, cs, b, off = st[1:6]
                c0, c1 = 128 * cs[0], 128 * (cs[-1] + 1)
                n = c1 - c0
                t0, t1 = ts[0], ts[-1] + 1
                src = banks[b][:, off : off + n * len(ts)].rearrange("p (t m) -> p t m", t=len(ts))
                nc.vector.scalar_tensor_tensor(out=y_unit(g, c0, c1)[:, t0:t1, :], in0=v_sb[g][:, t0:t1, c0:c1], scalar=1.5, in1=src,
                                               op0=ALU.mult, op1=ALU.subtract)
            elif k == "cast":
                e, g, m0, m1 = st[1], st[2], 32 * st[3], 32 * st[4]
                c0, c1 = 128 * st[5][0], 128 * (st[5][-1] + 1)
                src = y_unit(g, c0, c1)[:, :, m0 - c0 : m1 - c0].rearrange("p t m -> p m t")
                dst = y_il[:, g, 4 * m0 : 4 * m1].rearrange("p (m t) -> p m t", t=4)
                copy(e, dst, src)
            elif k == "qy":
                g, c0, c1 = st[1], 128 * st[2][0], 128 * (st[2][-1] + 1)
                nc.vector.quantize_mx(out=y_codes[:, g, c0:c1].bitcast(FP8X4), scales=y_sc[:, g, c0:c1], in_=y_il[:, g, 4 * c0 : 4 * c1])
            elif k == "sty":
                g, ts, cs = st[2], st[3], st[4]
                c0, c1 = 128 * cs[0], 128 * (cs[-1] + 1)
                t0, t1 = ts[0], ts[-1] + 1
                dst = out_0[512 * g : 512 * (g + 1), :].rearrange("(p t) m -> p t m", t=4)
                eng[st[1]].dma_start(out=dst[:, t0:t1, c0:c1], in_=y_unit(g, c0, c1)[:, t0:t1, :])
            elif k == "stq":
                g, c0, c1 = st[2], 128 * st[3][0], 128 * (st[3][-1] + 1)
                dst = out_1[g].rearrange("p m t -> p (m t)").bitcast(I32)
                eng[st[1]].dma_start(out=dst[:, c0:c1], in_=y_codes[:, g, c0:c1].bitcast(I32))
            elif k == "sts":
                g0, g1, r = st[2][0], st[2][-1] + 1, st[3]
                dst = out_2.rearrange("g (q r) n -> r q g n", r=4)[r]
                eng[st[1]].dma_start(out=dst[:, g0:g1, :].bitcast(I32), in_=y_sc[r:128:32, g0:g1, :].bitcast(I32))
            else:
                raise ValueError(k)
